import numpy as np
import ml_dtypes


def mxq(x, axis, fmt="e4m3"):
    dtype, down = {"e4m3": (ml_dtypes.float8_e4m3fn, 7), "e5m2": (ml_dtypes.float8_e5m2, 14)}[fmt]
    v = np.moveaxis(np.asarray(x, np.float32).astype(ml_dtypes.bfloat16).astype(np.float64), axis, -1)
    blocks = v.reshape(v.shape[:-1] + (-1, 32))
    amax = np.abs(blocks).max(-1, keepdims=True)
    byte = np.maximum(np.where(amax > 0, np.frexp(amax)[1] - 1 + 127, 0) - down, 1)
    scale = np.exp2(byte - 127.0)
    codes = (blocks / scale).astype(np.float32).astype(dtype).astype(np.float64)
    return np.moveaxis((codes * scale).reshape(v.shape), -1, axis)


WIDE = False


def mx_kscale(k):
    if not WIDE:
        return np.ones(k)
    levels = np.array([24, -24, 12, -12, 0])
    if k % 512:
        return np.exp2(np.random.permutation(np.resize(levels, k // 32))).repeat(32)
    a = np.empty((k // 512, 16))
    for p in range(k // 512):
        a[p, :8] = np.random.permutation(np.resize(levels, 8))
        for g in range(8):
            far = levels[np.abs(levels - a[p, g]) >= 10]
            a[p, g + 8] = far[np.random.randint(len(far))]
    return np.exp2(a.ravel()).repeat(32)


def f64(x):
    return np.asarray(x).astype(np.float64)


def striped(idx):
    return np.tile(idx.reshape(-1, 16).T, (8, 1)).astype(np.uint16)


def unstriped(offs):
    return offs[:16].T.reshape(-1).astype(np.int64)


E2M1 = np.array([0.0, 0.5, 1.0, 1.5, 2.0, 3.0, 4.0, 6.0, -0.0, -0.5, -1.0, -1.5, -2.0, -3.0, -4.0, -6.0])


def pack_weight(w, fmt):
    k, n = w.shape
    w = f64(np.asarray(w, np.float32).astype(ml_dtypes.bfloat16)).reshape(k // 32, 32, n)
    amax = np.abs(w).max(1)
    if fmt == "e4m3":
        byte = np.frexp(amax)[1] - 1 + 127 - 7
    else:
        mant, ex = np.frexp(amax / 6.0)
        byte = np.where(mant > 0.5, ex, ex - 1) + 127
    byte = np.clip(np.where(amax > 0, byte, 1), 1, 254)
    scaled = (w * np.exp2(127.0 - byte)[:, None, :]).reshape(k, n).astype(np.float32)
    by_word = np.ascontiguousarray(scaled.reshape(k // 512, 128, 4, n).transpose(0, 1, 3, 2))
    if fmt == "e4m3":
        words = by_word.astype(ml_dtypes.float8_e4m3fn).view(np.uint8)
    else:
        c = by_word.astype(ml_dtypes.float4_e2m1fn).view(np.uint8) & 0xF
        words = (c[..., 0::2] | (c[..., 1::2] << 4)).reshape(k // 512, 128, 2 * n)
    return np.ascontiguousarray(words), np.ascontiguousarray(byte.astype(np.uint8).reshape(k // 512, 16, n))


def unpack_weight(words, scales, fmt):
    g, _, n = scales.shape
    words = np.ascontiguousarray(words).reshape(g, 128, n, -1)
    if fmt == "e4m3":
        vals = words.view(ml_dtypes.float8_e4m3fn).astype(np.float64)
    else:
        nib = np.empty((g, 128, n, 4), np.uint8)
        nib[..., 0::2] = words & 0xF
        nib[..., 1::2] = words >> 4
        vals = E2M1[nib]
    vals = vals * np.repeat(np.exp2(scales.astype(np.float64) - 127.0), 8, axis=1)[..., None]
    return vals.transpose(0, 1, 3, 2).reshape(g * 512, n)


K, R, T, M, J = 512, 512, 2048, 512, 512


def setup_inputs():
    n = np.random.standard_normal
    s = mx_kscale(K)[:, None]
    u = mx_kscale(R)[:, None]
    p_tab = pack_weight(n((K, T)) * s, "e4m3")
    p_wa = pack_weight(n((K, R)) / np.sqrt(K) / s * u.T, "e4m3")
    p_wb = pack_weight(n((K, R)) / np.sqrt(K) / s / u.T, "e4m3")
    return {
        "tab_words": p_tab[0],
        "tab_scales": p_tab[1],
        "wa_words": p_wa[0],
        "wa_scales": p_wa[1],
        "wb_words": p_wb[0],
        "wb_scales": p_wb[1],
        "ts": np.tile(np.exp(0.5 * n(T)), (128, 1)).astype(np.float32),
        "offs": striped(np.random.permutation(T)[:M]),
        "offs2": striped(np.random.permutation(T)[:J]),
    }


def reference(tab_words, tab_scales, wa_words, wa_scales, wb_words, wb_scales, ts, offs, offs2):
    idx = unstriped(offs)
    idx2 = unstriped(offs2)
    tab_ = unpack_weight(tab_words, tab_scales, "e4m3")[:, idx]
    tabb_ = unpack_weight(tab_words, tab_scales, "e4m3")[:, idx2]
    wa_ = unpack_weight(wa_words, wa_scales, "e4m3")
    wb_ = unpack_weight(wb_words, wb_scales, "e4m3")
    za = wa_.T @ tab_
    zb = wb_.T @ tabb_
    ha = np.maximum(za, 0.0)
    hb = np.maximum(zb, 0.0)
    ha_ = mxq(ha, 0, "e4m3")
    hb_ = mxq(hb, 0, "e4m3")
    y = ha_.T @ hb_
    return y * 0.03125 * f64(ts)[0, idx2][None, :]

@@ -1,0 +1,177 @@
+from contextlib import ExitStack
+
+import concourse.mybir as mybir
+
+K, R, T, M, J = 512, 512, 2048, 512, 512
+FLOPS = 2 * K * R * M + 2 * K * R * J + 2 * R * M * J
+
+F32 = mybir.dt.float32
+BF16 = mybir.dt.bfloat16
+I32 = mybir.dt.int32
+U32 = mybir.dt.uint32
+U16 = mybir.dt.uint16
+U8 = mybir.dt.uint8
+FP8X4 = mybir.dt.float8_e4m3fn_x4
+MULT = mybir.AluOpType.mult
+RELU = mybir.ActivationFunctionType.Relu
+
+P = 128
+PACK = 4
+CH = 128
+NCH = 4
+HALF = 256
+OUT_SCALE = 0.03125
+
+
+def tile_list_biaff_relu_ts_kernel(
+    tc, tab_words, tab_scales, wa_words, wa_scales, wb_words, wb_scales, ts, offs, offs2, out
+):
+    nc = tc.nc
+    with ExitStack() as ctx:
+        keep = ctx.enter_context(tc.tile_pool(name="keep", bufs=1))
+        psum = ctx.enter_context(tc.psum_pool(name="psum", bufs=1))
+
+        def words_view(ap):
+            return ap[0].rearrange("p n i -> p (n i)").bitcast(I32)
+
+        def load_scale_rows(queues, dst, src):
+            for q in range(4):
+                queues[q].dma_start(out=dst[32 * q : 32 * q + 4, :].bitcast(I32), in_=src[0, 4 * q : 4 * q + 4, :].bitcast(I32))
+
+        list_a = keep.tile([P, M // 16], U16, name="list_a")
+        list_b = keep.tile([P, J // 16], U16, name="list_b")
+        tab_plane = keep.tile([P, T], U8, name="tab_plane", align_bytes=64)
+        wb_plane_raw = keep.tile([P, R], U8, name="wb_plane_raw", align_bytes=64)
+        wa_plane_raw = keep.tile([P, R], U8, name="wa_plane_raw", align_bytes=64)
+        wb_raw = keep.tile([P, R], I32, name="wb_raw", tag="wb_raw", align_bytes=64)
+        zeros_b = keep.tile([P, R // 4], I32, name="zeros_b", tag="table", align_bytes=64)
+        zeros_a = keep.tile([P, R // 4], I32, name="zeros_a", tag="wa_raw", align_bytes=64)
+        warm = keep.tile([P, 1], F32, name="warm")
+        warm_out = keep.tile([P, 1], F32, name="warm_out")
+
+        nc.vector.memset(tab_plane[:].bitcast(I32), 0)
+        nc.vector.memset(zeros_b[:], 0)
+        nc.vector.memset(warm[:], 0.0)
+        nc.vector.tensor_copy(out=wb_plane_raw[:].bitcast(I32), in_=zeros_b[:])
+        nc.vector.memset(zeros_a[:], 0)
+        nc.vector.tensor_copy(out=wa_plane_raw[:].bitcast(I32), in_=zeros_a[:])
+        table = keep.tile([P, T], I32, name="table", tag="table", align_bytes=64)
+        wa_raw = keep.tile([P, R], I32, name="wa_raw", tag="wa_raw", align_bytes=64)
+
+        nc.sync.dma_start(list_b[:], offs2)
+        nc.sync.dma_start(list_a[:], offs)
+        nc.scalar.dma_start(out=wb_raw[:], in_=words_view(wb_words))
+        load_scale_rows([nc.sync, nc.scalar, nc.sync, nc.scalar], tab_plane, tab_scales)
+        nc.scalar.activation(out=warm_out[:], in_=warm[:], func=RELU)
+        nc.sync.dma_start(out=table[:], in_=words_view(tab_words))
+        nc.sync.dma_start(out=wa_raw[:], in_=words_view(wa_words))
+        load_scale_rows([nc.scalar] * 4, wb_plane_raw, wb_scales)
+        load_scale_rows([nc.scalar] * 4, wa_plane_raw, wa_scales)
+
+        def deal_words(name, raw):
+            words = keep.tile([P, R], I32, name=name + "_dealt", align_bytes=64)
+            nc.vector.tensor_copy(
+                out=words[:].rearrange("p (t g i) -> p t g i", t=PACK, i=8),
+                in_=raw[:].rearrange("p (g t i) -> p t g i", t=PACK, i=8),
+            )
+            return words
+
+        def deal_plane(name, plane_raw):
+            plane = keep.tile([P, R], U8, name=name + "_plane", align_bytes=64)
+            nc.vector.tensor_copy(
+                out=plane[:].bitcast(I32).rearrange("p (t g i) -> p t g i", t=PACK, i=2),
+                in_=plane_raw[:].bitcast(I32).rearrange("p (g t i) -> p t g i", t=PACK, i=2),
+            )
+            return plane
+
+        wb_dealt = deal_words("wb", wb_raw)
+        ts_all = keep.tile([P, T], F32, name="ts_all", tag="wb_raw", align_bytes=64)
+        nc.sync.dma_start(out=ts_all[:], in_=ts)
+
+        vb_plane = keep.tile([P, J], U8, name="vb_plane", align_bytes=64)
+        va_plane = keep.tile([P, M], U8, name="va_plane", align_bytes=64)
+        vb_words = keep.tile([P, J], U32, name="vb_words", align_bytes=64)
+        va_words = keep.tile([P, M], U32, name="va_words", align_bytes=64)
+        nc.vector.tensor_copy(vb_plane[:], tab_plane[:].indirect(list_b[:]))
+        nc.vector.tensor_copy(va_plane[:], tab_plane[:].indirect(list_a[:]))
+
+        def gather_words(dst, lst, h):
+            nc.vector.tensor_copy(
+                dst[:, h * HALF : (h + 1) * HALF],
+                table[:].bitcast(U32).indirect(lst[:, h * HALF // 16 : (h + 1) * HALF // 16]),
+            )
+
+        def layer(c, tag, w_words, w_plane, v_words, v_plane, h_tile):
+            bank = psum.tile([P, PACK, CH], F32, name=tag, tag=tag)
+            cols = slice(c * CH, (c + 1) * CH)
+            for t in range(PACK):
+                wc = slice(t * P, (t + 1) * P)
+                nc.tensor.matmul_mx(
+                    out=bank[:, t, :],
+                    lhsT=w_words[:, wc].bitcast(FP8X4),
+                    lhsT_scale=w_plane[:, wc],
+                    rhs=v_words[:, cols].bitcast(FP8X4),
+                    rhs_scale=v_plane[:, cols],
+                    start=True,
+                    stop=True,
+                )
+            nc.scalar.activation(
+                out=h_tile[:, c * CH * PACK : (c + 1) * CH * PACK].rearrange("p (n t) -> p n t", t=PACK),
+                in_=bank[:].rearrange("p t n -> p n t"),
+                func=RELU,
+            )
+
+        hb = keep.tile([P, J * PACK], BF16, name="hb", align_bytes=64)
+        ha = keep.tile([P, M * PACK], BF16, name="ha", align_bytes=64)
+        hb_words = keep.tile([P, J], U32, name="hb_words", align_bytes=64)
+        ha_words = keep.tile([P, M], U32, name="ha_words", align_bytes=64)
+        hb_plane = keep.tile([P, J], U8, name="hb_plane", align_bytes=64)
+        ha_plane = keep.tile([P, M], U8, name="ha_plane", align_bytes=64)
+        ts_picked = keep.tile([P, J], F32, name="ts_picked", align_bytes=64)
+
+        def quantise(h_tile, words, plane, c0, c1):
+            nc.vector.quantize_mx(
+                out=words[:, c0:c1].bitcast(FP8X4), scales=plane[:, c0:c1], in_=h_tile[:, c0 * PACK : c1 * PACK]
+            )
+
+        gather_words(vb_words, list_b, 0)
+        wb_plane = deal_plane("wb", wb_plane_raw)
+        gather_words(vb_words, list_b, 1)
+        for c in range(NCH):
+            layer(c, "bank_b%d" % c, wb_dealt, wb_plane, vb_words, vb_plane, hb)
+        gather_words(va_words, list_a, 0)
+        wa_dealt = deal_words("wa", wa_raw)
+        wa_plane = deal_plane("wa", wa_plane_raw)
+        gather_words(va_words, list_a, 1)
+        for c in range(NCH):
+            layer(c, "bank_a%d" % c, wa_dealt, wa_plane, va_words, va_plane, ha)
+        quantise(hb, hb_words, hb_plane, 0, HALF)
+        nc.vector.tensor_copy(ts_picked[:], ts_all[:].indirect(list_b[:]))
+        quantise(hb, hb_words, hb_plane, HALF, J)
+
+        def score(c):
+            cols = slice(c * CH, (c + 1) * CH)
+            bank = psum.tile([P, J], F32, name="score%d" % c, tag="bank_b%d" % c)
+            nc.tensor.matmul_mx(
+                out=bank[:],
+                lhsT=ha_words[:, cols].bitcast(FP8X4),
+                lhsT_scale=ha_plane[:, cols],
+                rhs=hb_words[:].bitcast(FP8X4),
+                rhs_scale=hb_plane[:],
+                start=True,
+                stop=True,
+            )
+            return bank
+
+        def finish(c, bank):
+            res = keep.tile([P, J], F32, name="res%d" % c, align_bytes=64)
+            nc.vector.scalar_tensor_tensor(out=res[:], in0=bank[:], scalar=OUT_SCALE, in1=ts_picked[:], op0=MULT, op1=MULT)
+            nc.sync.dma_start(out=out[c * CH : (c + 1) * CH, :], in_=res[:])
+
+        banks = []
+        for c in range(NCH):
+            quantise(ha, ha_words, ha_plane, c * CH, (c + 1) * CH)
+            banks.append(score(c))
+            if c >= 1:
+                finish(c - 1, banks[c - 1])
+        finish(NCH - 1, banks[NCH - 1])

@@ -29,6 +29,8 @@ def tile_list_biaff_relu_ts_kernel(
     nc = tc.nc
     with ExitStack() as ctx:
         keep = ctx.enter_context(tc.tile_pool(name="keep", bufs=1))
+        stage = ctx.enter_context(tc.tile_pool(name="stage", bufs=1))
+        picked = ctx.enter_context(tc.tile_pool(name="picked", bufs=1))
         psum = ctx.enter_context(tc.psum_pool(name="psum", bufs=1))
 
         def words_view(ap):
@@ -40,12 +42,11 @@ def tile_list_biaff_relu_ts_kernel(
 
         list_a = keep.tile([P, M // 16], U16, name="list_a")
         list_b = keep.tile([P, J // 16], U16, name="list_b")
-        tab_plane = keep.tile([P, T], U8, name="tab_plane", align_bytes=64)
-        wb_plane_raw = keep.tile([P, R], U8, name="wb_plane_raw", align_bytes=64)
+        tab_plane = keep.tile([P, T], U8, name="tab_plane", tag="tab_plane", align_bytes=64)
+        wb_plane_raw = picked.tile([P, R], U8, name="wb_plane_raw", offset=4 * HALF - R // 2, align_bytes=64)
         wa_plane_raw = keep.tile([P, R], U8, name="wa_plane_raw", align_bytes=64)
-        wb_raw = keep.tile([P, R], I32, name="wb_raw", tag="wb_raw", align_bytes=64)
+        wb_raw = stage.tile([P, R], I32, name="wb_raw", offset=2 * R)
         zeros_b = keep.tile([P, R // 4], I32, name="zeros_b", tag="table", align_bytes=64)
-        zeros_a = keep.tile([P, R // 4], I32, name="zeros_a", tag="wa_raw", align_bytes=64)
         warm = keep.tile([P, 1], F32, name="warm")
         warm_out = keep.tile([P, 1], F32, name="warm_out")
 
@@ -53,10 +54,8 @@ def tile_list_biaff_relu_ts_kernel(
         nc.vector.memset(zeros_b[:], 0)
         nc.vector.memset(warm[:], 0.0)
         nc.vector.tensor_copy(out=wb_plane_raw[:].bitcast(I32), in_=zeros_b[:])
-        nc.vector.memset(zeros_a[:], 0)
-        nc.vector.tensor_copy(out=wa_plane_raw[:].bitcast(I32), in_=zeros_a[:])
+        nc.gpsimd.memset(wa_plane_raw[:].bitcast(I32), 0)
         table = keep.tile([P, T], I32, name="table", tag="table", align_bytes=64)
-        wa_raw = keep.tile([P, R], I32, name="wa_raw", tag="wa_raw", align_bytes=64)
 
         nc.sync.dma_start(list_b[:], offs2)
         nc.sync.dma_start(list_a[:], offs)
@@ -64,9 +63,7 @@ def tile_list_biaff_relu_ts_kernel(
         load_scale_rows([nc.sync, nc.scalar, nc.sync, nc.scalar], tab_plane, tab_scales)
         nc.scalar.activation(out=warm_out[:], in_=warm[:], func=RELU)
         nc.sync.dma_start(out=table[:], in_=words_view(tab_words))
-        nc.sync.dma_start(out=wa_raw[:], in_=words_view(wa_words))
-        load_scale_rows([nc.scalar] * 4, wb_plane_raw, wb_scales)
-        load_scale_rows([nc.scalar] * 4, wa_plane_raw, wa_scales)
+        load_scale_rows([nc.sync] * 4, wb_plane_raw, wb_scales)
 
         def deal_words(name, raw):
             words = keep.tile([P, R], I32, name=name + "_dealt", align_bytes=64)
@@ -76,28 +73,28 @@ def tile_list_biaff_relu_ts_kernel(
             )
             return words
 
-        def deal_plane(name, plane_raw):
-            plane = keep.tile([P, R], U8, name=name + "_plane", align_bytes=64)
+        def deal_plane(plane, plane_raw):
             nc.vector.tensor_copy(
                 out=plane[:].bitcast(I32).rearrange("p (t g i) -> p t g i", t=PACK, i=2),
                 in_=plane_raw[:].bitcast(I32).rearrange("p (g t i) -> p t g i", t=PACK, i=2),
             )
-            return plane
 
         wb_dealt = deal_words("wb", wb_raw)
-        ts_all = keep.tile([P, T], F32, name="ts_all", tag="wb_raw", align_bytes=64)
+        wa_raw = stage.tile([P, R], I32, name="wa_raw", offset=0)
+        ts_all = stage.tile([P, T], F32, name="ts_all", offset=4 * R)
+        nc.sync.dma_start(out=wa_raw[:], in_=words_view(wa_words))
+        load_scale_rows([nc.gpsimd, nc.gpsimd, nc.gpsimd, nc.gpsimd], wa_plane_raw, wa_scales)
         nc.sync.dma_start(out=ts_all[:], in_=ts)
 
         vb_plane = keep.tile([P, J], U8, name="vb_plane", align_bytes=64)
         va_plane = keep.tile([P, M], U8, name="va_plane", align_bytes=64)
-        vb_words = keep.tile([P, J], U32, name="vb_words", align_bytes=64)
-        va_words = keep.tile([P, M], U32, name="va_words", align_bytes=64)
+        vb_first = keep.tile([P, HALF], U32, name="vb_first", align_bytes=64)
         nc.vector.tensor_copy(vb_plane[:], tab_plane[:].indirect(list_b[:]))
         nc.vector.tensor_copy(va_plane[:], tab_plane[:].indirect(list_a[:]))
 
         def gather_words(dst, lst, h):
             nc.vector.tensor_copy(
-                dst[:, h * HALF : (h + 1) * HALF],
+                dst,
                 table[:].bitcast(U32).indirect(lst[:, h * HALF // 16 : (h + 1) * HALF // 16]),
             )
 
@@ -110,7 +107,7 @@ def tile_list_biaff_relu_ts_kernel(
                     out=bank[:, t, :],
                     lhsT=w_words[:, wc].bitcast(FP8X4),
                     lhsT_scale=w_plane[:, wc],
-                    rhs=v_words[:, cols].bitcast(FP8X4),
+                    rhs=v_words.bitcast(FP8X4),
                     rhs_scale=v_plane[:, cols],
                     start=True,
                     stop=True,
@@ -134,17 +131,21 @@ def tile_list_biaff_relu_ts_kernel(
                 out=words[:, c0:c1].bitcast(FP8X4), scales=plane[:, c0:c1], in_=h_tile[:, c0 * PACK : c1 * PACK]
             )
 
-        gather_words(vb_words, list_b, 0)
-        wb_plane = deal_plane("wb", wb_plane_raw)
-        gather_words(vb_words, list_b, 1)
+        gather_words(vb_first[:], list_b, 0)
+        wb_plane = keep.tile([P, R], U8, name="wb_plane", tag="tab_plane", align_bytes=64)
+        deal_plane(wb_plane, wb_plane_raw)
+        vb_second = picked.tile([P, HALF], U32, name="vb_second", offset=0, align_bytes=64)
+        va_words = picked.tile([P, M], U32, name="va_words", offset=4 * HALF, align_bytes=64)
+        gather_words(vb_second[:], list_b, 1)
         for c in range(NCH):
-            layer(c, "bank_b%d" % c, wb_dealt, wb_plane, vb_words, vb_plane, hb)
-        gather_words(va_words, list_a, 0)
+            layer(c, "bank_b%d" % c, wb_dealt, wb_plane, (vb_first, vb_second)[c // 2][:, (c % 2) * CH : (c % 2 + 1) * CH], vb_plane, hb)
+        gather_words(va_words[:, :HALF], list_a, 0)
         wa_dealt = deal_words("wa", wa_raw)
-        wa_plane = deal_plane("wa", wa_plane_raw)
-        gather_words(va_words, list_a, 1)
+        wa_plane = stage.tile([P, R], U8, name="wa_plane", offset=0, align_bytes=64)
+        deal_plane(wa_plane, wa_plane_raw)
+        gather_words(va_words[:, HALF:], list_a, 1)
         for c in range(NCH):
-            layer(c, "bank_a%d" % c, wa_dealt, wa_plane, va_words, va_plane, ha)
+            layer(c, "bank_a%d" % c, wa_dealt, wa_plane, va_words[:, c * CH : (c + 1) * CH], va_plane, ha)
         quantise(hb, hb_words, hb_plane, 0, HALF)
         nc.vector.tensor_copy(ts_picked[:], ts_all[:].indirect(list_b[:]))
         quantise(hb, hb_words, hb_plane, HALF, J)

@@ -54,7 +54,7 @@ def tile_list_biaff_relu_ts_kernel(
         nc.vector.memset(zeros_b[:], 0)
         nc.vector.memset(warm[:], 0.0)
         nc.vector.tensor_copy(out=wb_plane_raw[:].bitcast(I32), in_=zeros_b[:])
-        nc.gpsimd.memset(wa_plane_raw[:].bitcast(I32), 0)
+        nc.vector.memset(wa_plane_raw[:].bitcast(I32), 0)
         table = keep.tile([P, T], I32, name="table", tag="table", align_bytes=64)
 
         nc.sync.dma_start(list_b[:], offs2)
@@ -83,7 +83,7 @@ def tile_list_biaff_relu_ts_kernel(
         wa_raw = stage.tile([P, R], I32, name="wa_raw", offset=0)
         ts_all = stage.tile([P, T], F32, name="ts_all", offset=4 * R)
         nc.sync.dma_start(out=wa_raw[:], in_=words_view(wa_words))
-        load_scale_rows([nc.gpsimd, nc.gpsimd, nc.gpsimd, nc.gpsimd], wa_plane_raw, wa_scales)
+        load_scale_rows([nc.gpsimd, nc.gpsimd, nc.gpsimd, nc.sync], wa_plane_raw, wa_scales)
         nc.sync.dma_start(out=ts_all[:], in_=ts)
 
         vb_plane = keep.tile([P, J], U8, name="vb_plane", align_bytes=64)
@@ -120,8 +120,8 @@ def tile_list_biaff_relu_ts_kernel(
 
         hb = keep.tile([P, J * PACK], BF16, name="hb", align_bytes=64)
         ha = keep.tile([P, M * PACK], BF16, name="ha", align_bytes=64)
-        hb_words = keep.tile([P, J], U32, name="hb_words", align_bytes=64)
-        ha_words = keep.tile([P, M], U32, name="ha_words", align_bytes=64)
+        hb_words = stage.tile([P, J], U32, name="hb_words", offset=8 * R, align_bytes=64)
+        ha_words = stage.tile([P, M], U32, name="ha_words", offset=4 * R, align_bytes=64)
         hb_plane = keep.tile([P, J], U8, name="hb_plane", align_bytes=64)
         ha_plane = keep.tile([P, M], U8, name="ha_plane", align_bytes=64)
         ts_picked = keep.tile([P, J], F32, name="ts_picked", align_bytes=64)
@@ -140,15 +140,14 @@ def tile_list_biaff_relu_ts_kernel(
         for c in range(NCH):
             layer(c, "bank_b%d" % c, wb_dealt, wb_plane, (vb_first, vb_second)[c // 2][:, (c % 2) * CH : (c % 2 + 1) * CH], vb_plane, hb)
         gather_words(va_words[:, :HALF], list_a, 0)
+        gather_words(va_words[:, HALF:], list_a, 1)
         wa_dealt = deal_words("wa", wa_raw)
         wa_plane = stage.tile([P, R], U8, name="wa_plane", offset=0, align_bytes=64)
         deal_plane(wa_plane, wa_plane_raw)
-        gather_words(va_words[:, HALF:], list_a, 1)
         for c in range(NCH):
             layer(c, "bank_a%d" % c, wa_dealt, wa_plane, va_words[:, c * CH : (c + 1) * CH], va_plane, ha)
-        quantise(hb, hb_words, hb_plane, 0, HALF)
         nc.vector.tensor_copy(ts_picked[:], ts_all[:].indirect(list_b[:]))
-        quantise(hb, hb_words, hb_plane, HALF, J)
+        quantise(hb, hb_words, hb_plane, 0, J)
 
         def score(c):
             cols = slice(c * CH, (c + 1) * CH)
@@ -164,10 +163,14 @@ def tile_list_biaff_relu_ts_kernel(
             )
             return bank
 
-        def finish(c, bank):
+        def finish(c, bank, parts=1):
             res = keep.tile([P, J], F32, name="res%d" % c, align_bytes=64)
-            nc.vector.scalar_tensor_tensor(out=res[:], in0=bank[:], scalar=OUT_SCALE, in1=ts_picked[:], op0=MULT, op1=MULT)
-            nc.sync.dma_start(out=out[c * CH : (c + 1) * CH, :], in_=res[:])
+            for i in range(parts):
+                cols = slice(i * J // parts, (i + 1) * J // parts)
+                nc.vector.scalar_tensor_tensor(
+                    out=res[:, cols], in0=bank[:, cols], scalar=OUT_SCALE, in1=ts_picked[:, cols], op0=MULT, op1=MULT
+                )
+                (nc.sync, nc.scalar)[i].dma_start(out=out[c * CH : (c + 1) * CH, cols], in_=res[:, cols])
 
         banks = []
         for c in range(NCH):
@@ -175,4 +178,4 @@ def tile_list_biaff_relu_ts_kernel(
             banks.append(score(c))
             if c >= 1:
                 finish(c - 1, banks[c - 1])
-        finish(NCH - 1, banks[NCH - 1])
+        finish(NCH - 1, banks[NCH - 1], parts=2)

@@ -47,12 +47,9 @@ def tile_list_biaff_relu_ts_kernel(
         wa_plane_raw = keep.tile([P, R], U8, name="wa_plane_raw", align_bytes=64)
         wb_raw = stage.tile([P, R], I32, name="wb_raw", offset=2 * R)
         zeros_b = keep.tile([P, R // 4], I32, name="zeros_b", tag="table", align_bytes=64)
-        warm = keep.tile([P, 1], F32, name="warm")
-        warm_out = keep.tile([P, 1], F32, name="warm_out")
 
         nc.vector.memset(tab_plane[:].bitcast(I32), 0)
         nc.vector.memset(zeros_b[:], 0)
-        nc.vector.memset(warm[:], 0.0)
         nc.vector.tensor_copy(out=wb_plane_raw[:].bitcast(I32), in_=zeros_b[:])
         nc.vector.memset(wa_plane_raw[:].bitcast(I32), 0)
         table = keep.tile([P, T], I32, name="table", tag="table", align_bytes=64)
@@ -61,7 +58,6 @@ def tile_list_biaff_relu_ts_kernel(
         nc.sync.dma_start(list_a[:], offs)
         nc.scalar.dma_start(out=wb_raw[:], in_=words_view(wb_words))
         load_scale_rows([nc.sync, nc.scalar, nc.sync, nc.scalar], tab_plane, tab_scales)
-        nc.scalar.activation(out=warm_out[:], in_=warm[:], func=RELU)
         nc.sync.dma_start(out=table[:], in_=words_view(tab_words))
         load_scale_rows([nc.sync] * 4, wb_plane_raw, wb_scales)
 

@@ -21,6 +21,7 @@ CH = 128
 NCH = 4
 HALF = 256
 OUT_SCALE = 0.03125
+H_BYTES = CH * PACK * 2
 
 
 def tile_list_biaff_relu_ts_kernel(
@@ -31,6 +32,7 @@ def tile_list_biaff_relu_ts_kernel(
         keep = ctx.enter_context(tc.tile_pool(name="keep", bufs=1))
         stage = ctx.enter_context(tc.tile_pool(name="stage", bufs=1))
         picked = ctx.enter_context(tc.tile_pool(name="picked", bufs=1))
+        acts = ctx.enter_context(tc.tile_pool(name="acts", bufs=1))
         psum = ctx.enter_context(tc.psum_pool(name="psum", bufs=1))
 
         def words_view(ap):
@@ -48,10 +50,11 @@ def tile_list_biaff_relu_ts_kernel(
         wb_raw = stage.tile([P, R], I32, name="wb_raw", offset=2 * R)
         zeros_b = keep.tile([P, R // 4], I32, name="zeros_b", tag="table", align_bytes=64)
 
+        nc.vector.memset(wa_plane_raw[:96, :].bitcast(I32), 0)
         nc.vector.memset(tab_plane[:].bitcast(I32), 0)
         nc.vector.memset(zeros_b[:], 0)
+        nc.vector.memset(wa_plane_raw[96:, :].bitcast(I32), 0)
         nc.vector.tensor_copy(out=wb_plane_raw[:].bitcast(I32), in_=zeros_b[:])
-        nc.vector.memset(wa_plane_raw[:].bitcast(I32), 0)
         table = keep.tile([P, T], I32, name="table", tag="table", align_bytes=64)
 
         nc.sync.dma_start(list_b[:], offs2)
@@ -61,13 +64,11 @@ def tile_list_biaff_relu_ts_kernel(
         nc.sync.dma_start(out=table[:], in_=words_view(tab_words))
         load_scale_rows([nc.sync] * 4, wb_plane_raw, wb_scales)
 
-        def deal_words(name, raw):
-            words = keep.tile([P, R], I32, name=name + "_dealt", align_bytes=64)
+        def deal_words(words, raw):
             nc.vector.tensor_copy(
                 out=words[:].rearrange("p (t g i) -> p t g i", t=PACK, i=8),
                 in_=raw[:].rearrange("p (g t i) -> p t g i", t=PACK, i=8),
             )
-            return words
 
         def deal_plane(plane, plane_raw):
             nc.vector.tensor_copy(
@@ -75,7 +76,8 @@ def tile_list_biaff_relu_ts_kernel(
                 in_=plane_raw[:].bitcast(I32).rearrange("p (g t i) -> p t g i", t=PACK, i=2),
             )
 
-        wb_dealt = deal_words("wb", wb_raw)
+        wb_dealt = keep.tile([P, R], I32, name="wb_dealt", align_bytes=64)
+        deal_words(wb_dealt, wb_raw)
         wa_raw = stage.tile([P, R], I32, name="wa_raw", offset=0)
         ts_all = stage.tile([P, T], F32, name="ts_all", offset=4 * R)
         nc.sync.dma_start(out=wa_raw[:], in_=words_view(wa_words))
@@ -88,13 +90,13 @@ def tile_list_biaff_relu_ts_kernel(
         nc.vector.tensor_copy(vb_plane[:], tab_plane[:].indirect(list_b[:]))
         nc.vector.tensor_copy(va_plane[:], tab_plane[:].indirect(list_a[:]))
 
-        def gather_words(dst, lst, h):
-            nc.vector.tensor_copy(
-                dst,
-                table[:].bitcast(U32).indirect(lst[:, h * HALF // 16 : (h + 1) * HALF // 16]),
-            )
+        def half_of(lst, h):
+            return lst[:, h * HALF // 16 : (h + 1) * HALF // 16]
 
-        def layer(c, tag, w_words, w_plane, v_words, v_plane, h_tile):
+        def gather_words(dst, lst, h):
+            nc.vector.tensor_copy(dst, table[:].bitcast(U32).indirect(half_of(lst, h)))
+
+        def layer(c, tag, w_words, w_plane, v_words, v_plane, h_chunk):
             bank = psum.tile([P, PACK, CH], F32, name=tag, tag=tag)
             cols = slice(c * CH, (c + 1) * CH)
             for t in range(PACK):
@@ -109,44 +111,50 @@ def tile_list_biaff_relu_ts_kernel(
                     stop=True,
                 )
             nc.scalar.activation(
-                out=h_tile[:, c * CH * PACK : (c + 1) * CH * PACK].rearrange("p (n t) -> p n t", t=PACK),
+                out=h_chunk.rearrange("p (n t) -> p n t", t=PACK),
                 in_=bank[:].rearrange("p t n -> p n t"),
                 func=RELU,
             )
 
-        hb = keep.tile([P, J * PACK], BF16, name="hb", align_bytes=64)
-        ha = keep.tile([P, M * PACK], BF16, name="ha", align_bytes=64)
-        hb_words = stage.tile([P, J], U32, name="hb_words", offset=8 * R, align_bytes=64)
-        ha_words = stage.tile([P, M], U32, name="ha_words", offset=4 * R, align_bytes=64)
+        hb = [keep.tile([P, HALF * PACK], BF16, name="hb%d" % h, align_bytes=64) for h in range(2)]
+        ha = [acts.tile([P, CH * PACK], BF16, name="ha%d" % c, offset=c * H_BYTES, align_bytes=64) for c in range(NCH)]
+        hb_words = keep.tile([P, J], U32, name="hb_words", align_bytes=64)
+        ha_words = keep.tile([P, M], U32, name="ha_words", align_bytes=64)
         hb_plane = keep.tile([P, J], U8, name="hb_plane", align_bytes=64)
         ha_plane = keep.tile([P, M], U8, name="ha_plane", align_bytes=64)
-        ts_picked = keep.tile([P, J], F32, name="ts_picked", align_bytes=64)
 
         def quantise(h_tile, words, plane, c0, c1):
-            nc.vector.quantize_mx(
-                out=words[:, c0:c1].bitcast(FP8X4), scales=plane[:, c0:c1], in_=h_tile[:, c0 * PACK : c1 * PACK]
-            )
+            nc.vector.quantize_mx(out=words[:, c0:c1].bitcast(FP8X4), scales=plane[:, c0:c1], in_=h_tile[:])
 
         gather_words(vb_first[:], list_b, 0)
         wb_plane = keep.tile([P, R], U8, name="wb_plane", tag="tab_plane", align_bytes=64)
         deal_plane(wb_plane, wb_plane_raw)
         vb_second = picked.tile([P, HALF], U32, name="vb_second", offset=0, align_bytes=64)
-        va_words = picked.tile([P, M], U32, name="va_words", offset=4 * HALF, align_bytes=64)
         gather_words(vb_second[:], list_b, 1)
         for c in range(NCH):
-            layer(c, "bank_b%d" % c, wb_dealt, wb_plane, (vb_first, vb_second)[c // 2][:, (c % 2) * CH : (c % 2 + 1) * CH], vb_plane, hb)
+            half, part = divmod(c, 2)
+            layer(
+                c,
+                "bank_b%d" % c,
+                wb_dealt,
+                wb_plane,
+                (vb_first, vb_second)[half][:, part * CH : (part + 1) * CH],
+                vb_plane,
+                hb[half][:, part * CH * PACK : (part + 1) * CH * PACK],
+            )
+        wa_dealt = picked.tile([P, R], I32, name="wa_dealt", offset=4 * HALF, align_bytes=64)
+        deal_words(wa_dealt, wa_raw)
+        wa_plane = keep.tile([P, R], U8, name="wa_plane", align_bytes=64)
+        deal_plane(wa_plane, wa_plane_raw)
+        va_words = stage.tile([P, M], U32, name="va_words", offset=0, align_bytes=64)
         gather_words(va_words[:, :HALF], list_a, 0)
         gather_words(va_words[:, HALF:], list_a, 1)
-        wa_dealt = deal_words("wa", wa_raw)
-        wa_plane = stage.tile([P, R], U8, name="wa_plane", offset=0, align_bytes=64)
-        deal_plane(wa_plane, wa_plane_raw)
         for c in range(NCH):
-            layer(c, "bank_a%d" % c, wa_dealt, wa_plane, va_words[:, c * CH : (c + 1) * CH], va_plane, ha)
-        nc.vector.tensor_copy(ts_picked[:], ts_all[:].indirect(list_b[:]))
-        quantise(hb, hb_words, hb_plane, 0, J)
+            layer(c, "bank_a%d" % c, wa_dealt, wa_plane, va_words[:, c * CH : (c + 1) * CH], va_plane, ha[c][:])
 
         def score(c):
             cols = slice(c * CH, (c + 1) * CH)
+            quantise(ha[c], ha_words, ha_plane, c * CH, (c + 1) * CH)
             bank = psum.tile([P, J], F32, name="score%d" % c, tag="bank_b%d" % c)
             nc.tensor.matmul_mx(
                 out=bank[:],
@@ -159,8 +167,12 @@ def tile_list_biaff_relu_ts_kernel(
             )
             return bank
 
-        def finish(c, bank, parts=1):
-            res = keep.tile([P, J], F32, name="res%d" % c, align_bytes=64)
+        ts_picked = acts.tile([P, J], F32, name="TSP", offset=8 * H_BYTES, align_bytes=64)
+
+        def gather_ts(h):
+            nc.vector.tensor_copy(ts_picked[:, h * HALF : (h + 1) * HALF], ts_all[:].indirect(half_of(list_b, h)))
+
+        def finish(c, bank, res, parts=1):
             for i in range(parts):
                 cols = slice(i * J // parts, (i + 1) * J // parts)
                 nc.vector.scalar_tensor_tensor(
@@ -168,10 +180,19 @@ def tile_list_biaff_relu_ts_kernel(
                 )
                 (nc.sync, nc.scalar)[i].dma_start(out=out[c * CH : (c + 1) * CH, cols], in_=res[:, cols])
 
-        banks = []
-        for c in range(NCH):
-            quantise(ha, ha_words, ha_plane, c * CH, (c + 1) * CH)
-            banks.append(score(c))
-            if c >= 1:
-                finish(c - 1, banks[c - 1])
-        finish(NCH - 1, banks[NCH - 1], parts=2)
+        quantise(hb[0], hb_words, hb_plane, 0, HALF)
+        gather_ts(0)
+        quantise(hb[1], hb_words, hb_plane, HALF, J)
+        banks = [score(0)]
+        gather_ts(1)
+        banks.append(score(1))
+        banks.append(score(2))
+        res0 = acts.tile([P, J], F32, name="res0", offset=H_BYTES, align_bytes=64)
+        finish(0, banks[0], res0)
+        banks.append(score(3))
+        res1 = acts.tile([P, J], F32, name="res1", offset=3 * H_BYTES, align_bytes=64)
+        finish(1, banks[1], res1)
+        res2 = keep.tile([P, J], F32, name="res2", align_bytes=64)
+        finish(2, banks[2], res2)
+        res3 = keep.tile([P, J], F32, name="res3", align_bytes=64)
+        finish(3, banks[3], res3, parts=2)

@@ -30,8 +30,7 @@ def tile_list_biaff_relu_ts_kernel(
     nc = tc.nc
     with ExitStack() as ctx:
         keep = ctx.enter_context(tc.tile_pool(name="keep", bufs=1))
-        stage = ctx.enter_context(tc.tile_pool(name="stage", bufs=1))
-        picked = ctx.enter_context(tc.tile_pool(name="picked", bufs=1))
+        shared = ctx.enter_context(tc.tile_pool(name="shared", bufs=1))
         acts = ctx.enter_context(tc.tile_pool(name="acts", bufs=1))
         psum = ctx.enter_context(tc.psum_pool(name="psum", bufs=1))
 
@@ -44,69 +43,70 @@ def tile_list_biaff_relu_ts_kernel(
 
         list_a = keep.tile([P, M // 16], U16, name="list_a")
         list_b = keep.tile([P, J // 16], U16, name="list_b")
-        tab_plane = keep.tile([P, T], U8, name="tab_plane", tag="tab_plane", align_bytes=64)
-        wb_plane_raw = picked.tile([P, R], U8, name="wb_plane_raw", offset=4 * HALF - R // 2, align_bytes=64)
-        wa_plane_raw = keep.tile([P, R], U8, name="wa_plane_raw", align_bytes=64)
-        wb_raw = stage.tile([P, R], I32, name="wb_raw", offset=2 * R)
-        zeros_b = keep.tile([P, R // 4], I32, name="zeros_b", tag="table", align_bytes=64)
+        tab_plane = keep.tile([P, T], U8, name="tab_plane", align_bytes=64)
+        wa_plane_raw = shared.tile([P, R], U8, name="wa_plane_raw", tag="hb", align_bytes=64)
+        wb_plane_raw = keep.tile([P, R], U8, name="wb_plane_raw", align_bytes=64)
+        wb_raw = keep.tile([P, R], I32, name="wb_raw", align_bytes=64)
 
-        nc.vector.memset(wa_plane_raw[:96, :].bitcast(I32), 0)
-        nc.vector.memset(tab_plane[:].bitcast(I32), 0)
-        nc.vector.memset(zeros_b[:], 0)
+        nc.gpsimd.memset(wa_plane_raw[:96, :].bitcast(I32), 0)
+        with tc.tile_pool(name="early", bufs=1) as early:
+            zeros = early.tile([P, R // 4], I32, name="zeros", align_bytes=64)
+            nc.vector.memset(zeros[:], 0)
+            nc.vector.memset(tab_plane[:].bitcast(I32), 0)
+            nc.vector.tensor_copy(out=wb_plane_raw[:].bitcast(I32), in_=zeros[:])
         nc.vector.memset(wa_plane_raw[96:, :].bitcast(I32), 0)
-        nc.vector.tensor_copy(out=wb_plane_raw[:].bitcast(I32), in_=zeros_b[:])
-        table = keep.tile([P, T], I32, name="table", tag="table", align_bytes=64)
+        late = ctx.enter_context(tc.tile_pool(name="late", bufs=1))
+        table = late.tile([P, T], I32, name="table", align_bytes=64)
+        wa_raw = late.tile([P, R], I32, name="wa_raw", align_bytes=64)
+        ts_all = late.tile([P, T], F32, name="ts_all", tag="ts", align_bytes=64)
 
         nc.sync.dma_start(list_b[:], offs2)
-        nc.sync.dma_start(list_a[:], offs)
         nc.scalar.dma_start(out=wb_raw[:], in_=words_view(wb_words))
+        nc.sync.dma_start(list_a[:], offs)
         load_scale_rows([nc.sync, nc.scalar, nc.sync, nc.scalar], tab_plane, tab_scales)
         nc.sync.dma_start(out=table[:], in_=words_view(tab_words))
         load_scale_rows([nc.sync] * 4, wb_plane_raw, wb_scales)
 
-        def deal_words(words, raw):
-            nc.vector.tensor_copy(
-                out=words[:].rearrange("p (t g i) -> p t g i", t=PACK, i=8),
-                in_=raw[:].rearrange("p (g t i) -> p t g i", t=PACK, i=8),
-            )
-
-        def deal_plane(plane, plane_raw):
-            nc.vector.tensor_copy(
-                out=plane[:].bitcast(I32).rearrange("p (t g i) -> p t g i", t=PACK, i=2),
-                in_=plane_raw[:].bitcast(I32).rearrange("p (g t i) -> p t g i", t=PACK, i=2),
+        def deal(dst, src, run):
+            nc.scalar.copy(
+                out=dst[:].bitcast(U32).rearrange("p (t g i) -> p t g i", t=PACK, i=run),
+                in_=src[:].bitcast(U32).rearrange("p (g t i) -> p t g i", t=PACK, i=run),
             )
 
         wb_dealt = keep.tile([P, R], I32, name="wb_dealt", align_bytes=64)
-        deal_words(wb_dealt, wb_raw)
-        wa_raw = stage.tile([P, R], I32, name="wa_raw", offset=0)
-        ts_all = stage.tile([P, T], F32, name="ts_all", offset=4 * R)
+        deal(wb_dealt, wb_raw, 8)
         nc.sync.dma_start(out=wa_raw[:], in_=words_view(wa_words))
         load_scale_rows([nc.gpsimd, nc.gpsimd, nc.gpsimd, nc.sync], wa_plane_raw, wa_scales)
         nc.sync.dma_start(out=ts_all[:], in_=ts)
+        wb_plane = keep.tile([P, R], U8, name="wb_plane", align_bytes=64)
+        deal(wb_plane, wb_plane_raw, 2)
 
         vb_plane = keep.tile([P, J], U8, name="vb_plane", align_bytes=64)
         va_plane = keep.tile([P, M], U8, name="va_plane", align_bytes=64)
-        vb_first = keep.tile([P, HALF], U32, name="vb_first", align_bytes=64)
-        nc.vector.tensor_copy(vb_plane[:], tab_plane[:].indirect(list_b[:]))
-        nc.vector.tensor_copy(va_plane[:], tab_plane[:].indirect(list_a[:]))
+        vb_words = [keep.tile([P, HALF], U32, name="vb_words%d" % h, align_bytes=64) for h in range(2)]
+        va_words = [keep.tile([P, HALF], U32, name="va_words%d" % h, align_bytes=64) for h in range(2)]
 
         def half_of(lst, h):
             return lst[:, h * HALF // 16 : (h + 1) * HALF // 16]
 
-        def gather_words(dst, lst, h):
-            nc.vector.tensor_copy(dst, table[:].bitcast(U32).indirect(half_of(lst, h)))
+        nc.vector.tensor_copy(vb_plane[:], tab_plane[:].indirect(list_b[:]))
+        for h in range(2):
+            nc.vector.tensor_copy(vb_words[h][:], table[:].bitcast(U32).indirect(half_of(list_b, h)))
+        nc.vector.tensor_copy(va_plane[:], tab_plane[:].indirect(list_a[:]))
+        for h in range(2):
+            nc.vector.tensor_copy(va_words[h][:], table[:].bitcast(U32).indirect(half_of(list_a, h)))
 
         def layer(c, tag, w_words, w_plane, v_words, v_plane, h_chunk):
             bank = psum.tile([P, PACK, CH], F32, name=tag, tag=tag)
-            cols = slice(c * CH, (c + 1) * CH)
+            half, part = divmod(c, 2)
             for t in range(PACK):
                 wc = slice(t * P, (t + 1) * P)
                 nc.tensor.matmul_mx(
                     out=bank[:, t, :],
                     lhsT=w_words[:, wc].bitcast(FP8X4),
                     lhsT_scale=w_plane[:, wc],
-                    rhs=v_words.bitcast(FP8X4),
-                    rhs_scale=v_plane[:, cols],
+                    rhs=v_words[half][:, part * CH : (part + 1) * CH].bitcast(FP8X4),
+                    rhs_scale=v_plane[:, c * CH : (c + 1) * CH],
                     start=True,
                     stop=True,
                 )
@@ -116,41 +116,28 @@ def tile_list_biaff_relu_ts_kernel(
                 func=RELU,
             )
 
-        hb = [keep.tile([P, HALF * PACK], BF16, name="hb%d" % h, align_bytes=64) for h in range(2)]
         ha = [acts.tile([P, CH * PACK], BF16, name="ha%d" % c, offset=c * H_BYTES, align_bytes=64) for c in range(NCH)]
-        hb_words = keep.tile([P, J], U32, name="hb_words", align_bytes=64)
         ha_words = keep.tile([P, M], U32, name="ha_words", align_bytes=64)
         hb_plane = keep.tile([P, J], U8, name="hb_plane", align_bytes=64)
         ha_plane = keep.tile([P, M], U8, name="ha_plane", align_bytes=64)
+        wa_dealt = keep.tile([P, R], I32, name="wa_dealt", align_bytes=64)
+        wa_plane = keep.tile([P, R], U8, name="wa_plane", align_bytes=64)
+
+        deal(wa_dealt, wa_raw, 8)
+        deal(wa_plane, wa_plane_raw, 2)
+        hb = shared.tile([P, J * PACK], BF16, name="hb", tag="hb", align_bytes=64)
+        for c in range(NCH):
+            layer(c, "bank_b%d" % c, wb_dealt, wb_plane, vb_words, vb_plane, hb[:, c * CH * PACK : (c + 1) * CH * PACK])
+        for c in range(NCH):
+            layer(c, "bank_a%d" % c, wa_dealt, wa_plane, va_words, va_plane, ha[c][:])
 
         def quantise(h_tile, words, plane, c0, c1):
             nc.vector.quantize_mx(out=words[:, c0:c1].bitcast(FP8X4), scales=plane[:, c0:c1], in_=h_tile[:])
 
-        gather_words(vb_first[:], list_b, 0)
-        wb_plane = keep.tile([P, R], U8, name="wb_plane", tag="tab_plane", align_bytes=64)
-        deal_plane(wb_plane, wb_plane_raw)
-        vb_second = picked.tile([P, HALF], U32, name="vb_second", offset=0, align_bytes=64)
-        gather_words(vb_second[:], list_b, 1)
-        for c in range(NCH):
-            half, part = divmod(c, 2)
-            layer(
-                c,
-                "bank_b%d" % c,
-                wb_dealt,
-                wb_plane,
-                (vb_first, vb_second)[half][:, part * CH : (part + 1) * CH],
-                vb_plane,
-                hb[half][:, part * CH * PACK : (part + 1) * CH * PACK],
-            )
-        wa_dealt = picked.tile([P, R], I32, name="wa_dealt", offset=4 * HALF, align_bytes=64)
-        deal_words(wa_dealt, wa_raw)
-        wa_plane = keep.tile([P, R], U8, name="wa_plane", align_bytes=64)
-        deal_plane(wa_plane, wa_plane_raw)
-        va_words = stage.tile([P, M], U32, name="va_words", offset=0, align_bytes=64)
-        gather_words(va_words[:, :HALF], list_a, 0)
-        gather_words(va_words[:, HALF:], list_a, 1)
-        for c in range(NCH):
-            layer(c, "bank_a%d" % c, wa_dealt, wa_plane, va_words[:, c * CH : (c + 1) * CH], va_plane, ha[c][:])
+        ts_picked = keep.tile([P, J], F32, name="ts_picked", align_bytes=64)
+        nc.vector.tensor_copy(ts_picked[:], ts_all[:].indirect(list_b[:]))
+        hb_words = late.tile([P, J], U32, name="hb_words", tag="ts", align_bytes=64)
+        quantise(hb, hb_words, hb_plane, 0, J)
 
         def score(c):
             cols = slice(c * CH, (c + 1) * CH)
@@ -167,11 +154,6 @@ def tile_list_biaff_relu_ts_kernel(
             )
             return bank
 
-        ts_picked = acts.tile([P, J], F32, name="TSP", offset=8 * H_BYTES, align_bytes=64)
-
-        def gather_ts(h):
-            nc.vector.tensor_copy(ts_picked[:, h * HALF : (h + 1) * HALF], ts_all[:].indirect(half_of(list_b, h)))
-
         def finish(c, bank, res, parts=1):
             for i in range(parts):
                 cols = slice(i * J // parts, (i + 1) * J // parts)
@@ -180,16 +162,9 @@ def tile_list_biaff_relu_ts_kernel(
                 )
                 (nc.sync, nc.scalar)[i].dma_start(out=out[c * CH : (c + 1) * CH, cols], in_=res[:, cols])
 
-        quantise(hb[0], hb_words, hb_plane, 0, HALF)
-        gather_ts(0)
-        quantise(hb[1], hb_words, hb_plane, HALF, J)
-        banks = [score(0)]
-        gather_ts(1)
-        banks.append(score(1))
-        banks.append(score(2))
+        banks = [score(c) for c in range(NCH)]
         res0 = acts.tile([P, J], F32, name="res0", offset=H_BYTES, align_bytes=64)
         finish(0, banks[0], res0)
-        banks.append(score(3))
         res1 = acts.tile([P, J], F32, name="res1", offset=3 * H_BYTES, align_bytes=64)
         finish(1, banks[1], res1)
         res2 = keep.tile([P, J], F32, name="res2", align_bytes=64)

@@ -21,7 +21,7 @@ CH = 128
 NCH = 4
 HALF = 256
 OUT_SCALE = 0.03125
-H_BYTES = CH * PACK * 2
+H_WORDS = CH * PACK // 2
 
 
 def tile_list_biaff_relu_ts_kernel(
@@ -31,7 +31,6 @@ def tile_list_biaff_relu_ts_kernel(
     with ExitStack() as ctx:
         keep = ctx.enter_context(tc.tile_pool(name="keep", bufs=1))
         shared = ctx.enter_context(tc.tile_pool(name="shared", bufs=1))
-        acts = ctx.enter_context(tc.tile_pool(name="acts", bufs=1))
         psum = ctx.enter_context(tc.psum_pool(name="psum", bufs=1))
 
         def words_view(ap):
@@ -44,17 +43,16 @@ def tile_list_biaff_relu_ts_kernel(
         list_a = keep.tile([P, M // 16], U16, name="list_a")
         list_b = keep.tile([P, J // 16], U16, name="list_b")
         tab_plane = keep.tile([P, T], U8, name="tab_plane", align_bytes=64)
-        wa_plane_raw = shared.tile([P, R], U8, name="wa_plane_raw", tag="hb", align_bytes=64)
-        wb_plane_raw = keep.tile([P, R], U8, name="wb_plane_raw", align_bytes=64)
+        w_planes_raw = shared.tile([P, 2 * R], U8, name="w_planes_raw", tag="hb1", align_bytes=64)
+        wb_plane_raw = w_planes_raw[:, :R]
+        wa_plane_raw = w_planes_raw[:, R:]
         wb_raw = keep.tile([P, R], I32, name="wb_raw", align_bytes=64)
 
-        nc.gpsimd.memset(wa_plane_raw[:96, :].bitcast(I32), 0)
         with tc.tile_pool(name="early", bufs=1) as early:
-            zeros = early.tile([P, R // 4], I32, name="zeros", align_bytes=64)
-            nc.vector.memset(zeros[:], 0)
+            zeros = early.tile([P, R // 2], I32, name="zeros", align_bytes=64)
+            nc.gpsimd.memset(zeros[:], 0)
             nc.vector.memset(tab_plane[:].bitcast(I32), 0)
-            nc.vector.tensor_copy(out=wb_plane_raw[:].bitcast(I32), in_=zeros[:])
-        nc.vector.memset(wa_plane_raw[96:, :].bitcast(I32), 0)
+            nc.vector.tensor_copy(out=w_planes_raw[:].bitcast(I32), in_=zeros[:])
         late = ctx.enter_context(tc.tile_pool(name="late", bufs=1))
         table = late.tile([P, T], I32, name="table", align_bytes=64)
         wa_raw = late.tile([P, R], I32, name="wa_raw", align_bytes=64)
@@ -76,8 +74,8 @@ def tile_list_biaff_relu_ts_kernel(
         wb_dealt = keep.tile([P, R], I32, name="wb_dealt", align_bytes=64)
         deal(wb_dealt, wb_raw, 8)
         nc.sync.dma_start(out=wa_raw[:], in_=words_view(wa_words))
-        load_scale_rows([nc.gpsimd, nc.gpsimd, nc.gpsimd, nc.sync], wa_plane_raw, wa_scales)
         nc.sync.dma_start(out=ts_all[:], in_=ts)
+        load_scale_rows([nc.sync] * 4, wa_plane_raw, wa_scales)
         wb_plane = keep.tile([P, R], U8, name="wb_plane", align_bytes=64)
         deal(wb_plane, wb_plane_raw, 2)
 
@@ -116,7 +114,8 @@ def tile_list_biaff_relu_ts_kernel(
                 func=RELU,
             )
 
-        ha = [acts.tile([P, CH * PACK], BF16, name="ha%d" % c, offset=c * H_BYTES, align_bytes=64) for c in range(NCH)]
+        work = keep.tile([P, 5 * H_WORDS], F32, name="work", align_bytes=64)
+        ha = [work[:, s * H_WORDS : (s + 1) * H_WORDS].bitcast(BF16) for s in (0, 1, 2, 4)]
         ha_words = keep.tile([P, M], U32, name="ha_words", align_bytes=64)
         hb_plane = keep.tile([P, J], U8, name="hb_plane", align_bytes=64)
         ha_plane = keep.tile([P, M], U8, name="ha_plane", align_bytes=64)
@@ -125,11 +124,12 @@ def tile_list_biaff_relu_ts_kernel(
 
         deal(wa_dealt, wa_raw, 8)
         deal(wa_plane, wa_plane_raw, 2)
-        hb = shared.tile([P, J * PACK], BF16, name="hb", tag="hb", align_bytes=64)
+        hb = [shared.tile([P, HALF * PACK], BF16, name="hb%d" % h, tag="hb%d" % h, align_bytes=64) for h in range(2)]
         for c in range(NCH):
-            layer(c, "bank_b%d" % c, wb_dealt, wb_plane, vb_words, vb_plane, hb[:, c * CH * PACK : (c + 1) * CH * PACK])
+            half, part = divmod(c, 2)
+            layer(c, "bank_b%d" % c, wb_dealt, wb_plane, vb_words, vb_plane, hb[half][:, part * CH * PACK : (part + 1) * CH * PACK])
         for c in range(NCH):
-            layer(c, "bank_a%d" % c, wa_dealt, wa_plane, va_words, va_plane, ha[c][:])
+            layer(c, "bank_a%d" % c, wa_dealt, wa_plane, va_words, va_plane, ha[c])
 
         def quantise(h_tile, words, plane, c0, c1):
             nc.vector.quantize_mx(out=words[:, c0:c1].bitcast(FP8X4), scales=plane[:, c0:c1], in_=h_tile[:])
@@ -137,11 +137,15 @@ def tile_list_biaff_relu_ts_kernel(
         ts_picked = keep.tile([P, J], F32, name="ts_picked", align_bytes=64)
         nc.vector.tensor_copy(ts_picked[:], ts_all[:].indirect(list_b[:]))
         hb_words = late.tile([P, J], U32, name="hb_words", tag="ts", align_bytes=64)
-        quantise(hb, hb_words, hb_plane, 0, J)
+        for h in range(2):
+            quantise(hb[h], hb_words, hb_plane, h * HALF, (h + 1) * HALF)
 
         def score(c):
             cols = slice(c * CH, (c + 1) * CH)
-            quantise(ha[c], ha_words, ha_plane, c * CH, (c + 1) * CH)
+            parts = 2 if c >= 2 else 1
+            for i in range(parts):
+                c0, c1 = i * CH // parts, (i + 1) * CH // parts
+                quantise(ha[c][:, c0 * PACK : c1 * PACK], ha_words, ha_plane, c * CH + c0, c * CH + c1)
             bank = psum.tile([P, J], F32, name="score%d" % c, tag="bank_b%d" % c)
             nc.tensor.matmul_mx(
                 out=bank[:],
@@ -163,10 +167,8 @@ def tile_list_biaff_relu_ts_kernel(
                 (nc.sync, nc.scalar)[i].dma_start(out=out[c * CH : (c + 1) * CH, cols], in_=res[:, cols])
 
         banks = [score(c) for c in range(NCH)]
-        res0 = acts.tile([P, J], F32, name="res0", offset=H_BYTES, align_bytes=64)
-        finish(0, banks[0], res0)
-        res1 = acts.tile([P, J], F32, name="res1", offset=3 * H_BYTES, align_bytes=64)
-        finish(1, banks[1], res1)
+        for c in range(2):
+            finish(c, banks[c], work[:, H_WORDS // 2 + c * J : H_WORDS // 2 + (c + 1) * J])
         res2 = keep.tile([P, J], F32, name="res2", align_bytes=64)
         finish(2, banks[2], res2)
         res3 = keep.tile([P, J], F32, name="res3", align_bytes=64)

@@ -43,16 +43,16 @@ def tile_list_biaff_relu_ts_kernel(
         list_a = keep.tile([P, M // 16], U16, name="list_a")
         list_b = keep.tile([P, J // 16], U16, name="list_b")
         tab_plane = keep.tile([P, T], U8, name="tab_plane", align_bytes=64)
-        w_planes_raw = shared.tile([P, 2 * R], U8, name="w_planes_raw", tag="hb1", align_bytes=64)
-        wb_plane_raw = w_planes_raw[:, :R]
-        wa_plane_raw = w_planes_raw[:, R:]
+        wb_plane_raw = keep.tile([P, R], U8, name="wb_plane_raw", align_bytes=64)
+        wa_plane_raw = shared.tile([P, R], U8, name="wa_plane_raw", tag="hb1", align_bytes=64)
         wb_raw = keep.tile([P, R], I32, name="wb_raw", align_bytes=64)
 
         with tc.tile_pool(name="early", bufs=1) as early:
-            zeros = early.tile([P, R // 2], I32, name="zeros", align_bytes=64)
-            nc.gpsimd.memset(zeros[:], 0)
+            zeros = early.tile([P, R // 4], I32, name="zeros", align_bytes=64)
+            nc.vector.memset(zeros[:], 0)
             nc.vector.memset(tab_plane[:].bitcast(I32), 0)
-            nc.vector.tensor_copy(out=w_planes_raw[:].bitcast(I32), in_=zeros[:])
+            nc.vector.tensor_copy(out=wb_plane_raw[:].bitcast(I32), in_=zeros[:])
+        nc.vector.memset(wa_plane_raw[:].bitcast(I32), 0)
         late = ctx.enter_context(tc.tile_pool(name="late", bufs=1))
         table = late.tile([P, T], I32, name="table", align_bytes=64)
         wa_raw = late.tile([P, R], I32, name="wa_raw", align_bytes=64)

@@ -47,12 +47,13 @@ def tile_list_biaff_relu_ts_kernel(
         wa_plane_raw = shared.tile([P, R], U8, name="wa_plane_raw", tag="hb1", align_bytes=64)
         wb_raw = keep.tile([P, R], I32, name="wb_raw", align_bytes=64)
 
+        nc.vector.memset(wa_plane_raw[:96, :].bitcast(I32), 0)
+        nc.vector.memset(tab_plane[:].bitcast(I32), 0)
         with tc.tile_pool(name="early", bufs=1) as early:
             zeros = early.tile([P, R // 4], I32, name="zeros", align_bytes=64)
             nc.vector.memset(zeros[:], 0)
-            nc.vector.memset(tab_plane[:].bitcast(I32), 0)
+            nc.vector.memset(wa_plane_raw[96:, :].bitcast(I32), 0)
             nc.vector.tensor_copy(out=wb_plane_raw[:].bitcast(I32), in_=zeros[:])
-        nc.vector.memset(wa_plane_raw[:].bitcast(I32), 0)
         late = ctx.enter_context(tc.tile_pool(name="late", bufs=1))
         table = late.tile([P, T], I32, name="table", align_bytes=64)
         wa_raw = late.tile([P, R], I32, name="wa_raw", align_bytes=64)
@@ -74,8 +75,8 @@ def tile_list_biaff_relu_ts_kernel(
         wb_dealt = keep.tile([P, R], I32, name="wb_dealt", align_bytes=64)
         deal(wb_dealt, wb_raw, 8)
         nc.sync.dma_start(out=wa_raw[:], in_=words_view(wa_words))
+        load_scale_rows([nc.gpsimd, nc.gpsimd, nc.gpsimd, nc.sync], wa_plane_raw, wa_scales)
         nc.sync.dma_start(out=ts_all[:], in_=ts)
-        load_scale_rows([nc.sync] * 4, wa_plane_raw, wa_scales)
         wb_plane = keep.tile([P, R], U8, name="wb_plane", align_bytes=64)
         deal(wb_plane, wb_plane_raw, 2)
 

@@ -43,8 +43,8 @@ def tile_list_biaff_relu_ts_kernel(
         list_a = keep.tile([P, M // 16], U16, name="list_a")
         list_b = keep.tile([P, J // 16], U16, name="list_b")
         tab_plane = keep.tile([P, T], U8, name="tab_plane", align_bytes=64)
-        wb_plane_raw = keep.tile([P, R], U8, name="wb_plane_raw", align_bytes=64)
-        wa_plane_raw = shared.tile([P, R], U8, name="wa_plane_raw", tag="hb1", align_bytes=64)
+        wb_plane_raw = shared.tile([P, R], U8, name="wb_plane_raw", tag="wa_plane", align_bytes=64)
+        wa_plane_raw = shared.tile([P, R], U8, name="wa_plane_raw", tag="hb", align_bytes=64)
         wb_raw = keep.tile([P, R], I32, name="wb_raw", align_bytes=64)
 
         nc.vector.memset(wa_plane_raw[:96, :].bitcast(I32), 0)
@@ -55,9 +55,9 @@ def tile_list_biaff_relu_ts_kernel(
             nc.vector.memset(wa_plane_raw[96:, :].bitcast(I32), 0)
             nc.vector.tensor_copy(out=wb_plane_raw[:].bitcast(I32), in_=zeros[:])
         late = ctx.enter_context(tc.tile_pool(name="late", bufs=1))
-        table = late.tile([P, T], I32, name="table", align_bytes=64)
-        wa_raw = late.tile([P, R], I32, name="wa_raw", align_bytes=64)
-        ts_all = late.tile([P, T], F32, name="ts_all", tag="ts", align_bytes=64)
+        ts_all = late.tile([P, T], F32, name="ts_all", offset=0, align_bytes=64)
+        table = late.tile([P, T], I32, name="table", offset=4 * T, align_bytes=64)
+        wa_raw = late.tile([P, R], I32, name="wa_raw", offset=8 * T, align_bytes=64)
 
         nc.sync.dma_start(list_b[:], offs2)
         nc.scalar.dma_start(out=wb_raw[:], in_=words_view(wb_words))
@@ -82,29 +82,27 @@ def tile_list_biaff_relu_ts_kernel(
 
         vb_plane = keep.tile([P, J], U8, name="vb_plane", align_bytes=64)
         va_plane = keep.tile([P, M], U8, name="va_plane", align_bytes=64)
-        vb_words = [keep.tile([P, HALF], U32, name="vb_words%d" % h, align_bytes=64) for h in range(2)]
-        va_words = [keep.tile([P, HALF], U32, name="va_words%d" % h, align_bytes=64) for h in range(2)]
+        vb_words = keep.tile([P, J], U32, name="vb_words", align_bytes=64)
+        va_words = keep.tile([P, M], U32, name="va_words", align_bytes=64)
 
-        def half_of(lst, h):
-            return lst[:, h * HALF // 16 : (h + 1) * HALF // 16]
+        def gather_words(dst, lst, cuts):
+            for c0, c1 in zip(cuts, cuts[1:]):
+                nc.vector.tensor_copy(dst[:, c0:c1], table[:].bitcast(U32).indirect(lst[:, c0 // 16 : c1 // 16]))
 
         nc.vector.tensor_copy(vb_plane[:], tab_plane[:].indirect(list_b[:]))
-        for h in range(2):
-            nc.vector.tensor_copy(vb_words[h][:], table[:].bitcast(U32).indirect(half_of(list_b, h)))
+        gather_words(vb_words, list_b, (0, CH, HALF, J))
         nc.vector.tensor_copy(va_plane[:], tab_plane[:].indirect(list_a[:]))
-        for h in range(2):
-            nc.vector.tensor_copy(va_words[h][:], table[:].bitcast(U32).indirect(half_of(list_a, h)))
+        gather_words(va_words, list_a, (0, HALF, M))
 
         def layer(c, tag, w_words, w_plane, v_words, v_plane, h_chunk):
             bank = psum.tile([P, PACK, CH], F32, name=tag, tag=tag)
-            half, part = divmod(c, 2)
             for t in range(PACK):
                 wc = slice(t * P, (t + 1) * P)
                 nc.tensor.matmul_mx(
                     out=bank[:, t, :],
                     lhsT=w_words[:, wc].bitcast(FP8X4),
                     lhsT_scale=w_plane[:, wc],
-                    rhs=v_words[half][:, part * CH : (part + 1) * CH].bitcast(FP8X4),
+                    rhs=v_words[:, c * CH : (c + 1) * CH].bitcast(FP8X4),
                     rhs_scale=v_plane[:, c * CH : (c + 1) * CH],
                     start=True,
                     stop=True,
@@ -117,18 +115,17 @@ def tile_list_biaff_relu_ts_kernel(
 
         work = keep.tile([P, 5 * H_WORDS], F32, name="work", align_bytes=64)
         ha = [work[:, s * H_WORDS : (s + 1) * H_WORDS].bitcast(BF16) for s in (0, 1, 2, 4)]
-        ha_words = keep.tile([P, M], U32, name="ha_words", align_bytes=64)
+        ha_words = late.tile([P, M], U32, name="ha_words", offset=4 * J, align_bytes=64)
         hb_plane = keep.tile([P, J], U8, name="hb_plane", align_bytes=64)
         ha_plane = keep.tile([P, M], U8, name="ha_plane", align_bytes=64)
         wa_dealt = keep.tile([P, R], I32, name="wa_dealt", align_bytes=64)
-        wa_plane = keep.tile([P, R], U8, name="wa_plane", align_bytes=64)
+        wa_plane = shared.tile([P, R], U8, name="wa_plane", tag="wa_plane", align_bytes=64)
 
         deal(wa_dealt, wa_raw, 8)
         deal(wa_plane, wa_plane_raw, 2)
-        hb = [shared.tile([P, HALF * PACK], BF16, name="hb%d" % h, tag="hb%d" % h, align_bytes=64) for h in range(2)]
+        hb = shared.tile([P, J * PACK], BF16, name="hb", tag="hb", align_bytes=64)
         for c in range(NCH):
-            half, part = divmod(c, 2)
-            layer(c, "bank_b%d" % c, wb_dealt, wb_plane, vb_words, vb_plane, hb[half][:, part * CH * PACK : (part + 1) * CH * PACK])
+            layer(c, "bank_b%d" % c, wb_dealt, wb_plane, vb_words, vb_plane, hb[:, c * CH * PACK : (c + 1) * CH * PACK])
         for c in range(NCH):
             layer(c, "bank_a%d" % c, wa_dealt, wa_plane, va_words, va_plane, ha[c])
 
@@ -137,9 +134,9 @@ def tile_list_biaff_relu_ts_kernel(
 
         ts_picked = keep.tile([P, J], F32, name="ts_picked", align_bytes=64)
         nc.vector.tensor_copy(ts_picked[:], ts_all[:].indirect(list_b[:]))
-        hb_words = late.tile([P, J], U32, name="hb_words", tag="ts", align_bytes=64)
+        hb_words = late.tile([P, J], U32, name="hb_words", offset=0, align_bytes=64)
         for h in range(2):
-            quantise(hb[h], hb_words, hb_plane, h * HALF, (h + 1) * HALF)
+            quantise(hb[:, h * HALF * PACK : (h + 1) * HALF * PACK], hb_words, hb_plane, h * HALF, (h + 1) * HALF)
 
         def score(c):
             cols = slice(c * CH, (c + 1) * CH)

@@ -30,29 +30,28 @@ def tile_list_biaff_relu_ts_kernel(
     nc = tc.nc
     with ExitStack() as ctx:
         keep = ctx.enter_context(tc.tile_pool(name="keep", bufs=1))
-        shared = ctx.enter_context(tc.tile_pool(name="shared", bufs=1))
+        reused = ctx.enter_context(tc.tile_pool(name="reused", bufs=1))
         psum = ctx.enter_context(tc.psum_pool(name="psum", bufs=1))
 
         def words_view(ap):
             return ap[0].rearrange("p n i -> p (n i)").bitcast(I32)
 
-        def load_scale_rows(queues, dst, src):
+        def load_scale_rows(dst, src):
             for q in range(4):
-                queues[q].dma_start(out=dst[32 * q : 32 * q + 4, :].bitcast(I32), in_=src[0, 4 * q : 4 * q + 4, :].bitcast(I32))
+                nc.sync.dma_start(out=dst[32 * q : 32 * q + 4, :].bitcast(I32), in_=src[0, 4 * q : 4 * q + 4, :].bitcast(I32))
 
         list_a = keep.tile([P, M // 16], U16, name="list_a")
         list_b = keep.tile([P, J // 16], U16, name="list_b")
         tab_plane = keep.tile([P, T], U8, name="tab_plane", align_bytes=64)
-        wb_plane_raw = shared.tile([P, R], U8, name="wb_plane_raw", tag="wa_plane", align_bytes=64)
-        wa_plane_raw = shared.tile([P, R], U8, name="wa_plane_raw", tag="hb", align_bytes=64)
+        wb_plane_raw = keep.tile([P, R], U8, name="wb_plane_raw", align_bytes=64)
+        wa_plane_raw = reused.tile([P, R], U8, name="wa_plane_raw", offset=4 * J - R // 2, align_bytes=64)
         wb_raw = keep.tile([P, R], I32, name="wb_raw", align_bytes=64)
 
-        nc.vector.memset(wa_plane_raw[:96, :].bitcast(I32), 0)
         nc.vector.memset(tab_plane[:].bitcast(I32), 0)
         with tc.tile_pool(name="early", bufs=1) as early:
             zeros = early.tile([P, R // 4], I32, name="zeros", align_bytes=64)
             nc.vector.memset(zeros[:], 0)
-            nc.vector.memset(wa_plane_raw[96:, :].bitcast(I32), 0)
+            nc.vector.memset(wa_plane_raw[:].bitcast(I32), 0)
             nc.vector.tensor_copy(out=wb_plane_raw[:].bitcast(I32), in_=zeros[:])
         late = ctx.enter_context(tc.tile_pool(name="late", bufs=1))
         ts_all = late.tile([P, T], F32, name="ts_all", offset=0, align_bytes=64)
@@ -62,9 +61,9 @@ def tile_list_biaff_relu_ts_kernel(
         nc.sync.dma_start(list_b[:], offs2)
         nc.scalar.dma_start(out=wb_raw[:], in_=words_view(wb_words))
         nc.sync.dma_start(list_a[:], offs)
-        load_scale_rows([nc.sync, nc.scalar, nc.sync, nc.scalar], tab_plane, tab_scales)
+        load_scale_rows(tab_plane, tab_scales)
         nc.sync.dma_start(out=table[:], in_=words_view(tab_words))
-        load_scale_rows([nc.sync] * 4, wb_plane_raw, wb_scales)
+        load_scale_rows(wb_plane_raw, wb_scales)
 
         def deal(dst, src, run):
             nc.scalar.copy(
@@ -75,8 +74,8 @@ def tile_list_biaff_relu_ts_kernel(
         wb_dealt = keep.tile([P, R], I32, name="wb_dealt", align_bytes=64)
         deal(wb_dealt, wb_raw, 8)
         nc.sync.dma_start(out=wa_raw[:], in_=words_view(wa_words))
-        load_scale_rows([nc.gpsimd, nc.gpsimd, nc.gpsimd, nc.sync], wa_plane_raw, wa_scales)
         nc.sync.dma_start(out=ts_all[:], in_=ts)
+        load_scale_rows(wa_plane_raw, wa_scales)
         wb_plane = keep.tile([P, R], U8, name="wb_plane", align_bytes=64)
         deal(wb_plane, wb_plane_raw, 2)
 
@@ -113,34 +112,45 @@ def tile_list_biaff_relu_ts_kernel(
                 func=RELU,
             )
 
-        work = keep.tile([P, 5 * H_WORDS], F32, name="work", align_bytes=64)
-        ha = [work[:, s * H_WORDS : (s + 1) * H_WORDS].bitcast(BF16) for s in (0, 1, 2, 4)]
-        ha_words = late.tile([P, M], U32, name="ha_words", offset=4 * J, align_bytes=64)
+        base = J - H_WORDS // 2
+        ha_words = keep.tile([P, M], U32, name="ha_words", align_bytes=64)
         hb_plane = keep.tile([P, J], U8, name="hb_plane", align_bytes=64)
         ha_plane = keep.tile([P, M], U8, name="ha_plane", align_bytes=64)
         wa_dealt = keep.tile([P, R], I32, name="wa_dealt", align_bytes=64)
-        wa_plane = shared.tile([P, R], U8, name="wa_plane", tag="wa_plane", align_bytes=64)
+        wa_plane = keep.tile([P, R], U8, name="wa_plane", align_bytes=64)
 
         deal(wa_dealt, wa_raw, 8)
-        deal(wa_plane, wa_plane_raw, 2)
-        hb = shared.tile([P, J * PACK], BF16, name="hb", tag="hb", align_bytes=64)
+        nc.vector.tensor_copy(
+            out=wa_plane[:].bitcast(I32).rearrange("p (t g i) -> p t g i", t=PACK, i=2),
+            in_=wa_plane_raw[:].bitcast(I32).rearrange("p (g t i) -> p t g i", t=PACK, i=2),
+        )
+        work = reused.tile([P, base + 5 * H_WORDS], F32, name="work", offset=4 * J, align_bytes=64)
+        ha = [work[:, base + s * H_WORDS : base + (s + 1) * H_WORDS].bitcast(BF16) for s in (0, 1, 2, 4)]
+        hb = [keep.tile([P, HALF * PACK], BF16, name="hb%d" % h, align_bytes=64) for h in range(2)]
         for c in range(NCH):
-            layer(c, "bank_b%d" % c, wb_dealt, wb_plane, vb_words, vb_plane, hb[:, c * CH * PACK : (c + 1) * CH * PACK])
+            half, part = divmod(c, 2)
+            layer(c, "bank_b%d" % c, wb_dealt, wb_plane, vb_words, vb_plane, hb[half][:, part * CH * PACK : (part + 1) * CH * PACK])
         for c in range(NCH):
             layer(c, "bank_a%d" % c, wa_dealt, wa_plane, va_words, va_plane, ha[c])
 
         def quantise(h_tile, words, plane, c0, c1):
             nc.vector.quantize_mx(out=words[:, c0:c1].bitcast(FP8X4), scales=plane[:, c0:c1], in_=h_tile[:])
 
-        ts_picked = keep.tile([P, J], F32, name="ts_picked", align_bytes=64)
-        nc.vector.tensor_copy(ts_picked[:], ts_all[:].indirect(list_b[:]))
-        hb_words = late.tile([P, J], U32, name="hb_words", offset=0, align_bytes=64)
-        for h in range(2):
-            quantise(hb[:, h * HALF * PACK : (h + 1) * HALF * PACK], hb_words, hb_plane, h * HALF, (h + 1) * HALF)
+        ts_picked = work[:, :J]
+        hb_words = reused.tile([P, J], U32, name="hb_words", offset=0, align_bytes=64)
+
+        def gather_ts(h):
+            nc.vector.tensor_copy(
+                ts_picked[:, h * HALF : (h + 1) * HALF], ts_all[:].indirect(list_b[:, h * HALF // 16 : (h + 1) * HALF // 16])
+            )
+
+        quantise(hb[0], hb_words, hb_plane, 0, HALF)
+        gather_ts(0)
+        quantise(hb[1], hb_words, hb_plane, HALF, J)
 
         def score(c):
             cols = slice(c * CH, (c + 1) * CH)
-            parts = 2 if c >= 2 else 1
+            parts = 1 if c == 1 else 2
             for i in range(parts):
                 c0, c1 = i * CH // parts, (i + 1) * CH // parts
                 quantise(ha[c][:, c0 * PACK : c1 * PACK], ha_words, ha_plane, c * CH + c0, c * CH + c1)
@@ -164,9 +174,11 @@ def tile_list_biaff_relu_ts_kernel(
                 )
                 (nc.sync, nc.scalar)[i].dma_start(out=out[c * CH : (c + 1) * CH, cols], in_=res[:, cols])
 
-        banks = [score(c) for c in range(NCH)]
+        banks = [score(0)]
+        gather_ts(1)
+        banks.extend(score(c) for c in range(1, NCH))
         for c in range(2):
-            finish(c, banks[c], work[:, H_WORDS // 2 + c * J : H_WORDS // 2 + (c + 1) * J])
+            finish(c, banks[c], work[:, (c + 1) * J : (c + 2) * J])
         res2 = keep.tile([P, J], F32, name="res2", align_bytes=64)
         finish(2, banks[2], res2)
         res3 = keep.tile([P, J], F32, name="res3", align_bytes=64)

@@ -21,6 +21,7 @@ CH = 128
 NCH = 4
 HALF = 256
 OUT_SCALE = 0.03125
+TS_CUT = T - T // 8
 H_WORDS = CH * PACK // 2
 
 
@@ -74,8 +75,9 @@ def tile_list_biaff_relu_ts_kernel(
         wb_dealt = keep.tile([P, R], I32, name="wb_dealt", align_bytes=64)
         deal(wb_dealt, wb_raw, 8)
         nc.sync.dma_start(out=wa_raw[:], in_=words_view(wa_words))
-        nc.sync.dma_start(out=ts_all[:], in_=ts)
+        nc.sync.dma_start(out=ts_all[:, :TS_CUT], in_=ts[:, :TS_CUT])
         load_scale_rows(wa_plane_raw, wa_scales)
+        nc.sync.dma_start(out=ts_all[:, TS_CUT:], in_=ts[:, TS_CUT:])
         wb_plane = keep.tile([P, R], U8, name="wb_plane", align_bytes=64)
         deal(wb_plane, wb_plane_raw, 2)
 

@@ -21,7 +21,7 @@ CH = 128
 NCH = 4
 HALF = 256
 OUT_SCALE = 0.03125
-TS_CUT = T - T // 8
+TS_CUT = T - 3 * T // 16
 H_WORDS = CH * PACK // 2
 
 
@@ -37,8 +37,8 @@ def tile_list_biaff_relu_ts_kernel(
         def words_view(ap):
             return ap[0].rearrange("p n i -> p (n i)").bitcast(I32)
 
-        def load_scale_rows(dst, src):
-            for q in range(4):
+        def load_scale_rows(dst, src, quadrants=range(4)):
+            for q in quadrants:
                 nc.sync.dma_start(out=dst[32 * q : 32 * q + 4, :].bitcast(I32), in_=src[0, 4 * q : 4 * q + 4, :].bitcast(I32))
 
         list_a = keep.tile([P, M // 16], U16, name="list_a")
@@ -75,8 +75,9 @@ def tile_list_biaff_relu_ts_kernel(
         wb_dealt = keep.tile([P, R], I32, name="wb_dealt", align_bytes=64)
         deal(wb_dealt, wb_raw, 8)
         nc.sync.dma_start(out=wa_raw[:], in_=words_view(wa_words))
+        load_scale_rows(wa_plane_raw, wa_scales, range(1))
         nc.sync.dma_start(out=ts_all[:, :TS_CUT], in_=ts[:, :TS_CUT])
-        load_scale_rows(wa_plane_raw, wa_scales)
+        load_scale_rows(wa_plane_raw, wa_scales, range(1, 4))
         nc.sync.dma_start(out=ts_all[:, TS_CUT:], in_=ts[:, TS_CUT:])
         wb_plane = keep.tile([P, R], U8, name="wb_plane", align_bytes=64)
         deal(wb_plane, wb_plane_raw, 2)

@@ -39,7 +39,7 @@ def tile_list_biaff_relu_ts_kernel(
 
         def load_scale_rows(dst, src, quadrants=range(4)):
             for q in quadrants:
-                nc.sync.dma_start(out=dst[32 * q : 32 * q + 4, :].bitcast(I32), in_=src[0, 4 * q : 4 * q + 4, :].bitcast(I32))
+                nc.sync.dma_start(out=dst[q:P:32, :].bitcast(I32), in_=src[0, q:16:4, :].bitcast(I32))
 
         list_a = keep.tile([P, M // 16], U16, name="list_a")
         list_b = keep.tile([P, J // 16], U16, name="list_b")

@@ -22,7 +22,6 @@ NCH = 4
 HALF = 256
 OUT_SCALE = 0.03125
 TS_CUT = T - 3 * T // 16
-H_WORDS = CH * PACK // 2
 
 
 def tile_list_biaff_relu_ts_kernel(
@@ -96,7 +95,7 @@ def tile_list_biaff_relu_ts_kernel(
         nc.vector.tensor_copy(va_plane[:], tab_plane[:].indirect(list_a[:]))
         gather_words(va_words, list_a, (0, HALF, M))
 
-        def layer(c, tag, w_words, w_plane, v_words, v_plane, h_chunk):
+        def layer(c, tag, w_words, w_plane, v_words, v_plane, h_chunk, scale):
             bank = psum.tile([P, PACK, CH], F32, name=tag, tag=tag)
             for t in range(PACK):
                 wc = slice(t * P, (t + 1) * P)
@@ -113,10 +112,10 @@ def tile_list_biaff_relu_ts_kernel(
                 out=h_chunk.rearrange("p (n t) -> p n t", t=PACK),
                 in_=bank[:].rearrange("p t n -> p n t"),
                 func=RELU,
+                scale=scale,
             )
 
-        base = J - H_WORDS // 2
-        ha_words = keep.tile([P, M], U32, name="ha_words", align_bytes=64)
+        ha_words = [keep.tile([P, CH], U32, name="ha_words%d" % c, align_bytes=64) for c in range(NCH)]
         hb_plane = keep.tile([P, J], U8, name="hb_plane", align_bytes=64)
         ha_plane = keep.tile([P, M], U8, name="ha_plane", align_bytes=64)
         wa_dealt = keep.tile([P, R], I32, name="wa_dealt", align_bytes=64)
@@ -127,17 +126,19 @@ def tile_list_biaff_relu_ts_kernel(
             out=wa_plane[:].bitcast(I32).rearrange("p (t g i) -> p t g i", t=PACK, i=2),
             in_=wa_plane_raw[:].bitcast(I32).rearrange("p (g t i) -> p t g i", t=PACK, i=2),
         )
-        work = reused.tile([P, base + 5 * H_WORDS], F32, name="work", offset=4 * J, align_bytes=64)
-        ha = [work[:, base + s * H_WORDS : base + (s + 1) * H_WORDS].bitcast(BF16) for s in (0, 1, 2, 4)]
+        work = reused.tile([P, 3 * J], F32, name="work", offset=4 * J, align_bytes=64)
+        nc.vector.memset(work[:, HALF : 2 * J + 1 : HALF], OUT_SCALE)
+        factor = [work[:, k * HALF : k * HALF + 1] for k in range(1, NCH + 1)]
+        ha = [keep.tile([P, CH * PACK], BF16, name="ha%d" % c, align_bytes=64)[:] for c in range(NCH)]
         hb = [keep.tile([P, HALF * PACK], BF16, name="hb%d" % h, align_bytes=64) for h in range(2)]
         for c in range(NCH):
             half, part = divmod(c, 2)
-            layer(c, "bank_b%d" % c, wb_dealt, wb_plane, vb_words, vb_plane, hb[half][:, part * CH * PACK : (part + 1) * CH * PACK])
+            layer(c, "bank_b%d" % c, wb_dealt, wb_plane, vb_words, vb_plane, hb[half][:, part * CH * PACK : (part + 1) * CH * PACK], 1.0)
         for c in range(NCH):
-            layer(c, "bank_a%d" % c, wa_dealt, wa_plane, va_words, va_plane, ha[c])
+            layer(c, "bank_a%d" % c, wa_dealt, wa_plane, va_words, va_plane, ha[c], factor[c])
 
-        def quantise(h_tile, words, plane, c0, c1):
-            nc.vector.quantize_mx(out=words[:, c0:c1].bitcast(FP8X4), scales=plane[:, c0:c1], in_=h_tile[:])
+        def quantise(h_tile, words, plane):
+            nc.vector.quantize_mx(out=words.bitcast(FP8X4), scales=plane, in_=h_tile[:])
 
         ts_picked = work[:, :J]
         hb_words = reused.tile([P, J], U32, name="hb_words", offset=0, align_bytes=64)
@@ -147,20 +148,17 @@ def tile_list_biaff_relu_ts_kernel(
                 ts_picked[:, h * HALF : (h + 1) * HALF], ts_all[:].indirect(list_b[:, h * HALF // 16 : (h + 1) * HALF // 16])
             )
 
-        quantise(hb[0], hb_words, hb_plane, 0, HALF)
+        quantise(hb[0], hb_words[:, :HALF], hb_plane[:, :HALF])
         gather_ts(0)
-        quantise(hb[1], hb_words, hb_plane, HALF, J)
+        quantise(hb[1], hb_words[:, HALF:], hb_plane[:, HALF:])
 
         def score(c):
             cols = slice(c * CH, (c + 1) * CH)
-            parts = 1 if c == 1 else 2
-            for i in range(parts):
-                c0, c1 = i * CH // parts, (i + 1) * CH // parts
-                quantise(ha[c][:, c0 * PACK : c1 * PACK], ha_words, ha_plane, c * CH + c0, c * CH + c1)
+            quantise(ha[c], ha_words[c][:], ha_plane[:, cols])
             bank = psum.tile([P, J], F32, name="score%d" % c, tag="bank_b%d" % c)
             nc.tensor.matmul_mx(
                 out=bank[:],
-                lhsT=ha_words[:, cols].bitcast(FP8X4),
+                lhsT=ha_words[c][:].bitcast(FP8X4),
                 lhsT_scale=ha_plane[:, cols],
                 rhs=hb_words[:].bitcast(FP8X4),
                 rhs_scale=hb_plane[:],
@@ -172,16 +170,14 @@ def tile_list_biaff_relu_ts_kernel(
         def finish(c, bank, res, parts=1):
             for i in range(parts):
                 cols = slice(i * J // parts, (i + 1) * J // parts)
-                nc.vector.scalar_tensor_tensor(
-                    out=res[:, cols], in0=bank[:, cols], scalar=OUT_SCALE, in1=ts_picked[:, cols], op0=MULT, op1=MULT
-                )
+                nc.vector.tensor_tensor(out=res[:, cols], in0=bank[:, cols], in1=ts_picked[:, cols], op=MULT)
                 (nc.sync, nc.scalar)[i].dma_start(out=out[c * CH : (c + 1) * CH, cols], in_=res[:, cols])
 
         banks = [score(0)]
         gather_ts(1)
         banks.extend(score(c) for c in range(1, NCH))
-        for c in range(2):
-            finish(c, banks[c], work[:, (c + 1) * J : (c + 2) * J])
+        finish(0, banks[0], work[:, J : 2 * J], parts=2)
+        finish(1, banks[1], work[:, 2 * J :])
         res2 = keep.tile([P, J], F32, name="res2", align_bytes=64)
         finish(2, banks[2], res2)
         res3 = keep.tile([P, J], F32, name="res3", align_bytes=64)

@@ -58,8 +58,8 @@ def tile_list_biaff_relu_ts_kernel(
         table = late.tile([P, T], I32, name="table", offset=4 * T, align_bytes=64)
         wa_raw = late.tile([P, R], I32, name="wa_raw", offset=8 * T, align_bytes=64)
 
+        nc.sync.dma_start(out=wb_raw[:], in_=words_view(wb_words))
         nc.sync.dma_start(list_b[:], offs2)
-        nc.scalar.dma_start(out=wb_raw[:], in_=words_view(wb_words))
         nc.sync.dma_start(list_a[:], offs)
         load_scale_rows(tab_plane, tab_scales)
         nc.sync.dma_start(out=table[:], in_=words_view(tab_words))
@@ -152,33 +152,38 @@ def tile_list_biaff_relu_ts_kernel(
         gather_ts(0)
         quantise(hb[1], hb_words[:, HALF:], hb_plane[:, HALF:])
 
-        def score(c):
-            cols = slice(c * CH, (c + 1) * CH)
-            quantise(ha[c], ha_words[c][:], ha_plane[:, cols])
-            bank = psum.tile([P, J], F32, name="score%d" % c, tag="bank_b%d" % c)
-            nc.tensor.matmul_mx(
-                out=bank[:],
-                lhsT=ha_words[c][:].bitcast(FP8X4),
-                lhsT_scale=ha_plane[:, cols],
-                rhs=hb_words[:].bitcast(FP8X4),
-                rhs_scale=hb_plane[:],
-                start=True,
-                stop=True,
-            )
-            return bank
+        def score(c, tags):
+            rows = slice(c * CH, (c + 1) * CH)
+            quantise(ha[c], ha_words[c][:], ha_plane[:, rows])
+            width = J // len(tags)
+            parts = []
+            for i, tag in enumerate(tags):
+                cols = slice(i * width, (i + 1) * width)
+                bank = psum.tile([P, width], F32, name="score%d_%d" % (c, i), tag=tag)
+                nc.tensor.matmul_mx(
+                    out=bank[:],
+                    lhsT=ha_words[c][:].bitcast(FP8X4),
+                    lhsT_scale=ha_plane[:, rows],
+                    rhs=hb_words[:, cols].bitcast(FP8X4),
+                    rhs_scale=hb_plane[:, cols],
+                    start=True,
+                    stop=True,
+                )
+                parts.append(bank[:])
+            return parts
 
-        def finish(c, bank, res, parts=1):
-            for i in range(parts):
-                cols = slice(i * J // parts, (i + 1) * J // parts)
-                nc.vector.tensor_tensor(out=res[:, cols], in0=bank[:, cols], in1=ts_picked[:, cols], op=MULT)
+        def finish(c, parts, res):
+            for i, part in enumerate(parts):
+                cols = slice(i * J // len(parts), (i + 1) * J // len(parts))
+                nc.vector.tensor_tensor(out=res[:, cols], in0=part, in1=ts_picked[:, cols], op=MULT)
                 (nc.sync, nc.scalar)[i].dma_start(out=out[c * CH : (c + 1) * CH, cols], in_=res[:, cols])
 
-        banks = [score(0)]
+        banks = [score(0, ("bank_b0", "bank_a0"))]
         gather_ts(1)
-        banks.extend(score(c) for c in range(1, NCH))
-        finish(0, banks[0], work[:, J : 2 * J], parts=2)
+        banks.extend(score(c, ("bank_b%d" % c,)) for c in range(1, NCH))
+        finish(0, banks[0], work[:, J : 2 * J])
         finish(1, banks[1], work[:, 2 * J :])
         res2 = keep.tile([P, J], F32, name="res2", align_bytes=64)
         finish(2, banks[2], res2)
         res3 = keep.tile([P, J], F32, name="res3", align_bytes=64)
-        finish(3, banks[3], res3, parts=2)
+        finish(3, [banks[3][0][:, :HALF], banks[3][0][:, HALF:]], res3)

from contextlib import ExitStack

import concourse.mybir as mybir

K, R, T, M, J = 512, 512, 2048, 512, 512
FLOPS = 2 * K * R * M + 2 * K * R * J + 2 * R * M * J

F32 = mybir.dt.float32
BF16 = mybir.dt.bfloat16
I32 = mybir.dt.int32
U32 = mybir.dt.uint32
U16 = mybir.dt.uint16
U8 = mybir.dt.uint8
FP8X4 = mybir.dt.float8_e4m3fn_x4
MULT = mybir.AluOpType.mult
RELU = mybir.ActivationFunctionType.Relu

P = 128
PACK = 4
CH = 128
NCH = 4
HALF = 256
OUT_SCALE = 0.03125
TS_CUT = T - 3 * T // 16


def tile_list_biaff_relu_ts_kernel(
    tc, tab_words, tab_scales, wa_words, wa_scales, wb_words, wb_scales, ts, offs, offs2, out
):
    nc = tc.nc
    with ExitStack() as ctx:
        keep = ctx.enter_context(tc.tile_pool(name="keep", bufs=1))
        reused = ctx.enter_context(tc.tile_pool(name="reused", bufs=1))
        psum = ctx.enter_context(tc.psum_pool(name="psum", bufs=1))

        def words_view(ap):
            return ap[0].rearrange("p n i -> p (n i)").bitcast(I32)

        def load_scale_rows(dst, src, quadrants=range(4)):
            for q in quadrants:
                nc.sync.dma_start(out=dst[q:P:32, :].bitcast(I32), in_=src[0, q:16:4, :].bitcast(I32))

        list_a = keep.tile([P, M // 16], U16, name="list_a")
        list_b = keep.tile([P, J // 16], U16, name="list_b")
        tab_plane = keep.tile([P, T], U8, name="tab_plane", align_bytes=64)
        wb_plane_raw = keep.tile([P, R], U8, name="wb_plane_raw", align_bytes=64)
        wa_plane_raw = reused.tile([P, R], U8, name="wa_plane_raw", offset=4 * J - R // 2, align_bytes=64)
        wb_raw = keep.tile([P, R], I32, name="wb_raw", align_bytes=64)

        nc.vector.memset(tab_plane[:].bitcast(I32), 0)
        with tc.tile_pool(name="early", bufs=1) as early:
            zeros = early.tile([P, R // 4], I32, name="zeros", align_bytes=64)
            nc.vector.memset(zeros[:], 0)
            nc.vector.memset(wa_plane_raw[:].bitcast(I32), 0)
            nc.vector.tensor_copy(out=wb_plane_raw[:].bitcast(I32), in_=zeros[:])
        late = ctx.enter_context(tc.tile_pool(name="late", bufs=1))
        ts_all = late.tile([P, T], F32, name="ts_all", offset=0, align_bytes=64)
        table = late.tile([P, T], I32, name="table", offset=4 * T, align_bytes=64)
        wa_raw = late.tile([P, R], I32, name="wa_raw", offset=8 * T, align_bytes=64)

        nc.sync.dma_start(out=wb_raw[:], in_=words_view(wb_words))
        nc.sync.dma_start(list_b[:], offs2)
        nc.sync.dma_start(list_a[:], offs)
        load_scale_rows(tab_plane, tab_scales)
        nc.sync.dma_start(out=table[:], in_=words_view(tab_words))
        load_scale_rows(wb_plane_raw, wb_scales)

        def deal(dst, src, run):
            nc.scalar.copy(
                out=dst[:].bitcast(U32).rearrange("p (t g i) -> p t g i", t=PACK, i=run),
                in_=src[:].bitcast(U32).rearrange("p (g t i) -> p t g i", t=PACK, i=run),
            )

        wb_dealt = keep.tile([P, R], I32, name="wb_dealt", align_bytes=64)
        deal(wb_dealt, wb_raw, 8)
        nc.sync.dma_start(out=wa_raw[:], in_=words_view(wa_words))
        load_scale_rows(wa_plane_raw, wa_scales, range(1))
        nc.sync.dma_start(out=ts_all[:, :TS_CUT], in_=ts[:, :TS_CUT])
        load_scale_rows(wa_plane_raw, wa_scales, range(1, 4))
        nc.sync.dma_start(out=ts_all[:, TS_CUT:], in_=ts[:, TS_CUT:])
        wb_plane = keep.tile([P, R], U8, name="wb_plane", align_bytes=64)
        deal(wb_plane, wb_plane_raw, 2)

        vb_plane = keep.tile([P, J], U8, name="vb_plane", align_bytes=64)
        va_plane = keep.tile([P, M], U8, name="va_plane", align_bytes=64)
        vb_words = keep.tile([P, J], U32, name="vb_words", align_bytes=64)
        va_words = keep.tile([P, M], U32, name="va_words", align_bytes=64)

        def gather_words(dst, lst, cuts):
            for c0, c1 in zip(cuts, cuts[1:]):
                nc.vector.tensor_copy(dst[:, c0:c1], table[:].bitcast(U32).indirect(lst[:, c0 // 16 : c1 // 16]))

        nc.vector.tensor_copy(vb_plane[:], tab_plane[:].indirect(list_b[:]))
        gather_words(vb_words, list_b, (0, CH, HALF, J))
        nc.vector.tensor_copy(va_plane[:], tab_plane[:].indirect(list_a[:]))
        gather_words(va_words, list_a, (0, HALF, M))

        def layer(c, tag, w_words, w_plane, v_words, v_plane, h_chunk, scale):
            bank = psum.tile([P, PACK, CH], F32, name=tag, tag=tag)
            for t in range(PACK):
                wc = slice(t * P, (t + 1) * P)
                nc.tensor.matmul_mx(
                    out=bank[:, t, :],
                    lhsT=w_words[:, wc].bitcast(FP8X4),
                    lhsT_scale=w_plane[:, wc],
                    rhs=v_words[:, c * CH : (c + 1) * CH].bitcast(FP8X4),
                    rhs_scale=v_plane[:, c * CH : (c + 1) * CH],
                    start=True,
                    stop=True,
                )
            nc.scalar.activation(
                out=h_chunk.rearrange("p (n t) -> p n t", t=PACK),
                in_=bank[:].rearrange("p t n -> p n t"),
                func=RELU,
                scale=scale,
            )

        ha_words = [keep.tile([P, CH], U32, name="ha_words%d" % c, align_bytes=64) for c in range(NCH)]
        hb_plane = keep.tile([P, J], U8, name="hb_plane", align_bytes=64)
        ha_plane = keep.tile([P, M], U8, name="ha_plane", align_bytes=64)
        wa_dealt = keep.tile([P, R], I32, name="wa_dealt", align_bytes=64)
        wa_plane = keep.tile([P, R], U8, name="wa_plane", align_bytes=64)

        deal(wa_dealt, wa_raw, 8)
        nc.vector.tensor_copy(
            out=wa_plane[:].bitcast(I32).rearrange("p (t g i) -> p t g i", t=PACK, i=2),
            in_=wa_plane_raw[:].bitcast(I32).rearrange("p (g t i) -> p t g i", t=PACK, i=2),
        )
        work = reused.tile([P, 3 * J], F32, name="work", offset=4 * J, align_bytes=64)
        nc.vector.memset(work[:, HALF : 2 * J + 1 : HALF], OUT_SCALE)
        factor = [work[:, k * HALF : k * HALF + 1] for k in range(1, NCH + 1)]
        ha = [keep.tile([P, CH * PACK], BF16, name="ha%d" % c, align_bytes=64)[:] for c in range(NCH)]
        hb = [keep.tile([P, HALF * PACK], BF16, name="hb%d" % h, align_bytes=64) for h in range(2)]
        for c in range(NCH):
            half, part = divmod(c, 2)
            layer(c, "bank_b%d" % c, wb_dealt, wb_plane, vb_words, vb_plane, hb[half][:, part * CH * PACK : (part + 1) * CH * PACK], 1.0)
        for c in range(NCH):
            layer(c, "bank_a%d" % c, wa_dealt, wa_plane, va_words, va_plane, ha[c], factor[c])

        def quantise(h_tile, words, plane):
            nc.vector.quantize_mx(out=words.bitcast(FP8X4), scales=plane, in_=h_tile[:])

        ts_picked = work[:, :J]
        hb_words = reused.tile([P, J], U32, name="hb_words", offset=0, align_bytes=64)

        def gather_ts(h):
            nc.vector.tensor_copy(
                ts_picked[:, h * HALF : (h + 1) * HALF], ts_all[:].indirect(list_b[:, h * HALF // 16 : (h + 1) * HALF // 16])
            )

        quantise(hb[0], hb_words[:, :HALF], hb_plane[:, :HALF])
        gather_ts(0)
        quantise(hb[1], hb_words[:, HALF:], hb_plane[:, HALF:])

        def score(c, tags):
            rows = slice(c * CH, (c + 1) * CH)
            quantise(ha[c], ha_words[c][:], ha_plane[:, rows])
            width = J // len(tags)
            parts = []
            for i, tag in enumerate(tags):
                cols = slice(i * width, (i + 1) * width)
                bank = psum.tile([P, width], F32, name="score%d_%d" % (c, i), tag=tag)
                nc.tensor.matmul_mx(
                    out=bank[:],
                    lhsT=ha_words[c][:].bitcast(FP8X4),
                    lhsT_scale=ha_plane[:, rows],
                    rhs=hb_words[:, cols].bitcast(FP8X4),
                    rhs_scale=hb_plane[:, cols],
                    start=True,
                    stop=True,
                )
                parts.append(bank[:])
            return parts

        def finish(c, parts, res):
            for i, part in enumerate(parts):
                cols = slice(i * J // len(parts), (i + 1) * J // len(parts))
                nc.vector.tensor_tensor(out=res[:, cols], in0=part, in1=ts_picked[:, cols], op=MULT)
                (nc.sync, nc.scalar)[i].dma_start(out=out[c * CH : (c + 1) * CH, cols], in_=res[:, cols])

        banks = [score(0, ("bank_b0", "bank_a0"))]
        gather_ts(1)
        banks.extend(score(c, ("bank_b%d" % c,)) for c in range(1, NCH))
        finish(0, banks[0], work[:, J : 2 * J])
        finish(1, banks[1], work[:, 2 * J :])
        res2 = keep.tile([P, J], F32, name="res2", align_bytes=64)
        finish(2, banks[2], res2)
        res3 = keep.tile([P, J], F32, name="res3", align_bytes=64)
        finish(3, [banks[3][0][:, :HALF], banks[3][0][:, HALF:]], res3)
